import numpy as np
import ml_dtypes


def mxq(x, axis, fmt="e4m3"):
    dtype, down = {"e4m3": (ml_dtypes.float8_e4m3fn, 7), "e5m2": (ml_dtypes.float8_e5m2, 14)}[fmt]
    v = np.moveaxis(np.asarray(x, np.float32).astype(ml_dtypes.bfloat16).astype(np.float64), axis, -1)
    blocks = v.reshape(v.shape[:-1] + (-1, 32))
    amax = np.abs(blocks).max(-1, keepdims=True)
    byte = np.maximum(np.where(amax > 0, np.frexp(amax)[1] - 1 + 127, 0) - down, 1)
    scale = np.exp2(byte - 127.0)
    codes = (blocks / scale).astype(np.float32).astype(dtype).astype(np.float64)
    return np.moveaxis((codes * scale).reshape(v.shape), -1, axis)


WIDE = False


def mx_kscale(k):
    if not WIDE:
        return np.ones(k)
    levels = np.array([10, -10, 5, -5, 0])
    if k % 512:
        return np.exp2(np.random.permutation(np.resize(levels, k // 32))).repeat(32)
    a = np.empty((k // 512, 16))
    for p in range(k // 512):
        a[p, :8] = np.random.permutation(np.resize(levels, 8))
        for g in range(8):
            far = levels[np.abs(levels - a[p, g]) >= 10]
            a[p, g + 8] = far[np.random.randint(len(far))]
    return np.exp2(a.ravel()).repeat(32)


def f64(x):
    return np.asarray(x).astype(np.float64)


def striped(idx):
    return np.tile(idx.reshape(-1, 16).T, (8, 1)).astype(np.uint16)


def unstriped(offs):
    return offs[:16].T.reshape(-1).astype(np.int64)


def pack_weight(w):
    k, n = w.shape
    w = f64(np.asarray(w, np.float32).astype(ml_dtypes.bfloat16)).reshape(k // 32, 32, n)
    amax = np.abs(w).max(1)
    byte = np.clip(np.where(amax > 0, np.frexp(amax)[1] - 1 + 127 - 7, 1), 1, 254)
    scaled = (w * np.exp2(127.0 - byte)[:, None, :]).reshape(k, n).astype(np.float32)
    words = np.ascontiguousarray(scaled.reshape(k // 512, 128, 4, n).transpose(0, 1, 3, 2)).astype(ml_dtypes.float8_e4m3fn).view(np.uint8)
    return words, np.ascontiguousarray(byte.astype(np.uint8).reshape(k // 512, 16, n))


def unpack_weight(words, scales):
    g, p, n, _ = words.shape
    vals = np.ascontiguousarray(words).view(ml_dtypes.float8_e4m3fn).astype(np.float64) * np.repeat(np.exp2(scales.astype(np.float64) - 127.0), 8, axis=1)[..., None]
    return vals.transpose(0, 1, 3, 2).reshape(g * 512, n)


def relu(v):
    return np.maximum(v, 0.0)


K, T, S, H, N, D = 512, 2048, 512, 512, 256, 8


def setup_inputs():
    n = np.random.standard_normal
    s = mx_kscale(K)[:, None]
    u = mx_kscale(H)
    packed_xT = pack_weight(n((K, T)) * s)
    return {
        "x_words": packed_xT[0],
        "x_scales": packed_xT[1],
        "w1": (n((K, H)) / np.sqrt(K) / s).astype(np.float32),
        "w2": (n((H, N)) / np.sqrt(H) / u[:, None]).astype(np.float32),
        "gam": (np.random.uniform(0.5, 1.5, (H, 1)) * u[:, None]).astype(np.float32),
        "offs": striped(np.random.permutation(T)[:S]),
    }


def reference(x_words, x_scales, w1, w2, gam, offs):
    xq = unpack_weight(x_words, x_scales)[:, unstriped(offs)]
    y = mxq(f64(w1), 0, "e4m3").T @ xq
    my = y.reshape(len(y), -1, D).mean(axis=2)
    dd = y - np.repeat(my, D, axis=1)
    ee = (dd) ** 2
    ss = np.sqrt(ee.reshape(len(ee), -1, D).mean(axis=2) + 0.1)
    z = f64(gam) * (dd / np.repeat(ss, D, axis=1))
    return relu(mxq(f64(w2), 0, "e4m3").T @ mxq(z, 0, "e4m3"))

@@ -1,0 +1,164 @@
+from contextlib import ExitStack
+
+import concourse.mybir as mybir
+
+K, T, S, H, N, D = 512, 2048, 512, 512, 256, 8
+EPS = 0.1
+FLOPS = 2 * K * H * S + 2 * H * N * S
+
+F32 = mybir.dt.float32
+BF16 = mybir.dt.bfloat16
+I32 = mybir.dt.int32
+U32 = mybir.dt.uint32
+U16 = mybir.dt.uint16
+U8 = mybir.dt.uint8
+FP8X4 = mybir.dt.float8_e4m3fn_x4
+ALU = mybir.AluOpType
+ACT = mybir.ActivationFunctionType
+AX = mybir.AxisListType
+
+P = 128
+PACK = 4
+CHUNK = 128
+CHUNKS = S // CHUNK
+GROUPS = CHUNK // D
+HALF = S // 2
+W1_VECTOR = 96
+
+
+def tile_picked_ygrp_relu_p_kernel(tc, x_words, x_scales, w1, w2, gam, offs, out):
+    nc = tc.nc
+    with ExitStack() as ctx:
+        keep = ctx.enter_context(tc.tile_pool(name="keep", bufs=1))
+        psum = ctx.enter_context(tc.psum_pool(name="psum", bufs=1))
+
+        offsets = keep.tile([P, S // 16], U16, name="offsets")
+        table_words = keep.tile([P, T], U32, name="table_words", align_bytes=64)
+        table_scales = keep.tile([P, T], U8, name="table_scales", align_bytes=64)
+        w1_raw = keep.tile([P, PACK, H], F32, name="w1_raw", align_bytes=64)
+        w2_raw = keep.tile([P, PACK, N], F32, name="w2_raw", align_bytes=64)
+        gam_sb = keep.tile([P, PACK], F32, name="gam_sb")
+
+        nc.vector.memset(table_scales[:].bitcast(I32), 0)
+        nc.sync.dma_start(offsets[:], offs)
+        nc.sync.dma_start(out=w1_raw[:], in_=w1.rearrange("(p j) c -> p j c", j=PACK))
+        for q in range(4):
+            nc.sync.dma_start(out=table_scales[32 * q : 32 * q + 4, :].bitcast(I32),
+                              in_=x_scales[0, 4 * q : 4 * q + 4, :].bitcast(I32))
+        nc.sync.dma_start(out=table_words[:].bitcast(I32), in_=x_words[0].rearrange("p c r -> p (c r)").bitcast(I32))
+        nc.sync.dma_start(out=w2_raw[:], in_=w2.rearrange("(p j) c -> p j c", j=PACK))
+        nc.sync.dma_start(out=gam_sb[:], in_=gam.rearrange("(p t) o -> p (t o)", t=PACK))
+
+        w1_bf = keep.tile([P, PACK * P * PACK], BF16, name="w1_bf", align_bytes=64)
+        w1_dst = w1_bf[:].rearrange("p (t m j) -> p m j t", t=PACK, j=PACK)
+        w1_src = w1_raw[:].rearrange("p j (m t) -> p m j t", t=PACK)
+        nc.vector.tensor_copy(out=w1_dst[:, :W1_VECTOR], in_=w1_src[:, :W1_VECTOR])
+        nc.scalar.copy(out=w1_dst[:, W1_VECTOR:], in_=w1_src[:, W1_VECTOR:])
+
+        x_sc = keep.tile([P, S], U8, name="x_sc", align_bytes=64)
+        nc.vector.tensor_copy(x_sc[:], table_scales[:].indirect(offsets[:]))
+
+        w1_codes = keep.tile([P, H], U32, name="w1_codes", align_bytes=64)
+        w1_sc = keep.tile([P, H], U8, name="w1_sc", align_bytes=64)
+        nc.vector.quantize_mx(out=w1_codes[:].bitcast(FP8X4), scales=w1_sc[:], in_=w1_bf[:])
+
+        x_codes = []
+        for h in range(2):
+            g = keep.tile([P, HALF], U32, name=f"x_codes{h}", align_bytes=64)
+            nc.vector.tensor_copy(g[:], table_words[:].indirect(offsets[:, h * HALF // 16 : (h + 1) * HALF // 16]))
+            x_codes.append(g)
+
+        y = []
+        for u in range(CHUNKS):
+            bank = psum.tile([P, PACK, CHUNK], F32, name=f"y{u}")
+            c0 = u * CHUNK % HALF
+            for t in range(PACK):
+                nc.tensor.matmul_mx(
+                    out=bank[:, t, :],
+                    lhsT=w1_codes[:, t * P : (t + 1) * P].bitcast(FP8X4),
+                    lhsT_scale=w1_sc[:, t * P : (t + 1) * P],
+                    rhs=x_codes[u * CHUNK // HALF][:, c0 : c0 + CHUNK].bitcast(FP8X4),
+                    rhs_scale=x_sc[:, u * CHUNK : (u + 1) * CHUNK],
+                    start=True, stop=True,
+                )
+            y.append(bank)
+
+        w2_bf = keep.tile([P, N, PACK], BF16, name="w2_bf", align_bytes=64)
+        w2_codes = keep.tile([P, N], U32, name="w2_codes", align_bytes=64)
+        w2_sc = keep.tile([P, N], U8, name="w2_sc", align_bytes=64)
+
+        def w2_cast(h):
+            cols = slice(h * P, (h + 1) * P)
+            nc.scalar.copy(out=w2_bf[:, cols, :].rearrange("p (c i) j -> p c j i", i=4),
+                           in_=w2_raw[:, :, cols].rearrange("p j (c i) -> p c j i", i=4))
+
+        def w2_quantize():
+            nc.vector.quantize_mx(out=w2_codes[:].bitcast(FP8X4), scales=w2_sc[:],
+                                  in_=w2_bf[:].rearrange("p c j -> p (c j)"))
+
+        full = [P, GROUPS, D, PACK]
+        mean, dd, ee, rstd, factor, z = {}, {}, {}, {}, {}, {}
+
+        def group_mean(u):
+            total = keep.tile([P, GROUPS, PACK], F32, name=f"total{u}")
+            nc.vector.tensor_reduce(out=total[:], in_=y[u][:].rearrange("p t (v d) -> p v t d", d=D), axis=AX.X, op=ALU.add)
+            mean[u] = keep.tile([P, GROUPS, PACK], F32, name=f"mean{u}")
+            nc.scalar.activation(out=mean[u][:], in_=total[:], func=ACT.Copy, scale=1.0 / D)
+
+        def center(u):
+            dd[u] = keep.tile(full, F32, name=f"dd{u}")
+            nc.vector.tensor_tensor(out=dd[u][:], in0=y[u][:].rearrange("p t (v d) -> p v d t", d=D),
+                                    in1=mean[u][:].unsqueeze(2).broadcast_to(full), op=ALU.subtract)
+            ee[u] = keep.tile([P, GROUPS, PACK, D], F32, name=f"ee{u}")
+            nc.scalar.activation(out=ee[u][:].rearrange("p v t d -> p v d t"), in_=dd[u][:], func=ACT.Square)
+
+        def deviation(u):
+            sumsq = keep.tile([P, GROUPS, PACK], F32, name=f"sumsq{u}")
+            nc.vector.tensor_reduce(out=sumsq[:], in_=ee[u][:], axis=AX.X, op=ALU.add)
+            rstd[u] = keep.tile([P, GROUPS, PACK], F32, name=f"rstd{u}")
+            nc.scalar.activation(out=rstd[u][:], in_=sumsq[:], func=ACT.Abs_reciprocal_sqrt, scale=1.0 / D, bias=EPS)
+
+        def gain(u):
+            factor[u] = keep.tile([P, GROUPS, PACK], F32, name=f"factor{u}")
+            nc.vector.tensor_tensor(out=factor[u][:], in0=rstd[u][:],
+                                    in1=gam_sb[:].unsqueeze(1).broadcast_to([P, GROUPS, PACK]), op=ALU.mult)
+
+        def normalise(u):
+            z[u] = keep.tile(full, BF16, name=f"z{u}", align_bytes=64)
+            nc.vector.tensor_tensor(out=z[u][:], in0=dd[u][:], in1=factor[u][:].unsqueeze(2).broadcast_to(full), op=ALU.mult)
+
+        def second_layer(u):
+            z_codes = keep.tile([P, CHUNK], U32, name=f"z_codes{u}", align_bytes=64)
+            z_sc = keep.tile([P, CHUNK], U8, name=f"z_sc{u}", align_bytes=64)
+            nc.vector.quantize_mx(out=z_codes[:].bitcast(FP8X4), scales=z_sc[:], in_=z[u][:].rearrange("p v d t -> p (v d t)"))
+            acc = psum.tile([P, N // P, CHUNK], F32, name=f"acc{u}")
+            for h in range(N // P):
+                nc.tensor.matmul_mx(
+                    out=acc[:, h, :],
+                    lhsT=w2_codes[:, h * P : (h + 1) * P].bitcast(FP8X4),
+                    lhsT_scale=w2_sc[:, h * P : (h + 1) * P],
+                    rhs=z_codes[:].bitcast(FP8X4),
+                    rhs_scale=z_sc[:],
+                    start=True, stop=True,
+                )
+            res = keep.tile([P, N // P, CHUNK], F32, name=f"res{u}")
+            nc.scalar.activation(out=res[:], in_=acc[:], func=ACT.Relu)
+            nc.sync.dma_start(out=out.rearrange("(h p) j -> p h j", p=P)[:, :, u * CHUNK : (u + 1) * CHUNK], in_=res[:])
+
+        for step in range(CHUNKS + 4):
+            if step < CHUNKS:
+                group_mean(step)
+            if 1 <= step < CHUNKS + 1:
+                center(step - 1)
+            if step in (1, 2):
+                w2_cast(step - 1)
+            if 2 <= step < CHUNKS + 2:
+                deviation(step - 2)
+            if step == 3:
+                w2_quantize()
+            if 3 <= step < CHUNKS + 3:
+                gain(step - 3)
+            if 4 <= step:
+                second_layer(step - 4)
+            if 3 <= step < CHUNKS + 3:
+                normalise(step - 3)

@@ -1,6 +1,7 @@
 from contextlib import ExitStack
 
 import concourse.mybir as mybir
+from concourse.masks import make_identity
 
 K, T, S, H, N, D = 512, 2048, 512, 512, 256, 8
 EPS = 0.1
@@ -23,7 +24,7 @@ CHUNK = 128
 CHUNKS = S // CHUNK
 GROUPS = CHUNK // D
 HALF = S // 2
-W1_VECTOR = 96
+W1_VECTOR = 80
 
 
 def tile_picked_ygrp_relu_p_kernel(tc, x_words, x_scales, w1, w2, gam, offs, out):
@@ -39,9 +40,9 @@ def tile_picked_ygrp_relu_p_kernel(tc, x_words, x_scales, w1, w2, gam, offs, out
         w2_raw = keep.tile([P, PACK, N], F32, name="w2_raw", align_bytes=64)
         gam_sb = keep.tile([P, PACK], F32, name="gam_sb")
 
-        nc.vector.memset(table_scales[:].bitcast(I32), 0)
-        nc.sync.dma_start(offsets[:], offs)
+        nc.gpsimd.memset(table_scales[:].bitcast(I32), 0)
         nc.sync.dma_start(out=w1_raw[:], in_=w1.rearrange("(p j) c -> p j c", j=PACK))
+        nc.sync.dma_start(offsets[:], offs)
         for q in range(4):
             nc.sync.dma_start(out=table_scales[32 * q : 32 * q + 4, :].bitcast(I32),
                               in_=x_scales[0, 4 * q : 4 * q + 4, :].bitcast(I32))
@@ -49,18 +50,26 @@ def tile_picked_ygrp_relu_p_kernel(tc, x_words, x_scales, w1, w2, gam, offs, out
         nc.sync.dma_start(out=w2_raw[:], in_=w2.rearrange("(p j) c -> p j c", j=PACK))
         nc.sync.dma_start(out=gam_sb[:], in_=gam.rearrange("(p t) o -> p (t o)", t=PACK))
 
+        identity = keep.tile([P, P], F32, name="identity")
+        make_identity(nc, identity[:])
+
+        warm_in = keep.tile([P, 1], F32, name="warm_in")
+        warm_out = keep.tile([P, 1], F32, name="warm_out")
+        nc.vector.memset(warm_in[:], 1.0)
+        nc.scalar.activation(out=warm_out[:], in_=warm_in[:], func=ACT.Abs_reciprocal_sqrt)
+
         w1_bf = keep.tile([P, PACK * P * PACK], BF16, name="w1_bf", align_bytes=64)
-        w1_dst = w1_bf[:].rearrange("p (t m j) -> p m j t", t=PACK, j=PACK)
-        w1_src = w1_raw[:].rearrange("p j (m t) -> p m j t", t=PACK)
+        w1_dst = w1_bf[:].rearrange("p (t m j) -> p m t j", t=PACK, j=PACK)
+        w1_src = w1_raw[:].rearrange("p j (m t) -> p m t j", t=PACK)
         nc.vector.tensor_copy(out=w1_dst[:, :W1_VECTOR], in_=w1_src[:, :W1_VECTOR])
         nc.scalar.copy(out=w1_dst[:, W1_VECTOR:], in_=w1_src[:, W1_VECTOR:])
-
-        x_sc = keep.tile([P, S], U8, name="x_sc", align_bytes=64)
-        nc.vector.tensor_copy(x_sc[:], table_scales[:].indirect(offsets[:]))
 
         w1_codes = keep.tile([P, H], U32, name="w1_codes", align_bytes=64)
         w1_sc = keep.tile([P, H], U8, name="w1_sc", align_bytes=64)
         nc.vector.quantize_mx(out=w1_codes[:].bitcast(FP8X4), scales=w1_sc[:], in_=w1_bf[:])
+
+        x_sc = keep.tile([P, S], U8, name="x_sc", align_bytes=64)
+        nc.vector.tensor_copy(x_sc[:], table_scales[:].indirect(offsets[:]))
 
         x_codes = []
         for h in range(2):
@@ -70,7 +79,7 @@ def tile_picked_ygrp_relu_p_kernel(tc, x_words, x_scales, w1, w2, gam, offs, out
 
         y = []
         for u in range(CHUNKS):
-            bank = psum.tile([P, PACK, CHUNK], F32, name=f"y{u}")
+            bank = psum.tile([P, PACK, CHUNK], F32, name=f"y{u}", tag=f"bank{u}")
             c0 = u * CHUNK % HALF
             for t in range(PACK):
                 nc.tensor.matmul_mx(
@@ -83,82 +92,110 @@ def tile_picked_ygrp_relu_p_kernel(tc, x_words, x_scales, w1, w2, gam, offs, out
                 )
             y.append(bank)
 
-        w2_bf = keep.tile([P, N, PACK], BF16, name="w2_bf", align_bytes=64)
         w2_codes = keep.tile([P, N], U32, name="w2_codes", align_bytes=64)
         w2_sc = keep.tile([P, N], U8, name="w2_sc", align_bytes=64)
 
-        def w2_cast(h):
-            cols = slice(h * P, (h + 1) * P)
-            nc.scalar.copy(out=w2_bf[:, cols, :].rearrange("p (c i) j -> p c j i", i=4),
-                           in_=w2_raw[:, :, cols].rearrange("p j (c i) -> p c j i", i=4))
-
-        def w2_quantize():
-            nc.vector.quantize_mx(out=w2_codes[:].bitcast(FP8X4), scales=w2_sc[:],
-                                  in_=w2_bf[:].rearrange("p c j -> p (c j)"))
-
         full = [P, GROUPS, D, PACK]
-        mean, dd, ee, rstd, factor, z = {}, {}, {}, {}, {}, {}
+        mean, z_bf = {}, {}
+        dd = [keep.tile(full, F32, name=f"dd{u}") for u in range(CHUNKS)]
+        ee = {}
 
         def group_mean(u):
-            total = keep.tile([P, GROUPS, PACK], F32, name=f"total{u}")
+            total = keep.tile([P, GROUPS, PACK], F32, name=f"total{u}", tag=(f"stat{u - 2}" if u >= 2 else f"total{u}"), align_bytes=64)
             nc.vector.tensor_reduce(out=total[:], in_=y[u][:].rearrange("p t (v d) -> p v t d", d=D), axis=AX.X, op=ALU.add)
-            mean[u] = keep.tile([P, GROUPS, PACK], F32, name=f"mean{u}")
+            mean[u] = keep.tile([P, GROUPS, PACK], F32, name=f"mean{u}", tag=(f"stat{u}" if u < 2 else f"mean{u}"), align_bytes=64)
             nc.scalar.activation(out=mean[u][:], in_=total[:], func=ACT.Copy, scale=1.0 / D)
 
-        def center(u):
-            dd[u] = keep.tile(full, F32, name=f"dd{u}")
-            nc.vector.tensor_tensor(out=dd[u][:], in0=y[u][:].rearrange("p t (v d) -> p v d t", d=D),
-                                    in1=mean[u][:].unsqueeze(2).broadcast_to(full), op=ALU.subtract)
-            ee[u] = keep.tile([P, GROUPS, PACK, D], F32, name=f"ee{u}")
-            nc.scalar.activation(out=ee[u][:].rearrange("p v t d -> p v d t"), in_=dd[u][:], func=ACT.Square)
+        def center(pair):
+            half = [P, GROUPS, D // 2, PACK]
+            for h in range(2):
+                ee[pair, h] = keep.tile([P, D // 2, 2, GROUPS, PACK], F32, name=f"ee{pair}_{h}", tag=f"ee{(pair + h) % 2}")
+                for u in (2 * pair, 2 * pair + 1):
+                    members = y[u][:].rearrange("p t (v h d) -> p h v d t", h=2, d=D // 2)[:, h]
+                    nc.vector.tensor_tensor(out=dd[u][:, :, h * D // 2 : (h + 1) * D // 2], in0=members, in1=mean[u][:].unsqueeze(2).broadcast_to(half), op=ALU.subtract)
+                    nc.scalar.activation(out=ee[pair, h][:, :, u % 2].rearrange("p d v t -> p v d t"), in_=dd[u][:, :, h * D // 2 : (h + 1) * D // 2], func=ACT.Square)
 
-        def deviation(u):
-            sumsq = keep.tile([P, GROUPS, PACK], F32, name=f"sumsq{u}")
-            nc.vector.tensor_reduce(out=sumsq[:], in_=ee[u][:], axis=AX.X, op=ALU.add)
-            rstd[u] = keep.tile([P, GROUPS, PACK], F32, name=f"rstd{u}")
-            nc.scalar.activation(out=rstd[u][:], in_=sumsq[:], func=ACT.Abs_reciprocal_sqrt, scale=1.0 / D, bias=EPS)
+        def deviation(pair):
+            turned = psum.tile([P, P], F32, name=f"turned{pair}", tag=f"turned{pair}")
+            for d in range(D):
+                nc.tensor.matmul(out=turned[:], lhsT=ee[pair, d // 4][:, d % 4].rearrange("p u v t -> p (u v t)"), rhs=identity[:],
+                                 is_transpose=True, start=(d == 0), stop=(d == D - 1))
+            rstd_turned = keep.tile([P, P], F32, name=f"rstd_turned{pair}")
+            nc.scalar.activation(out=rstd_turned[:], in_=turned[:], func=ACT.Abs_reciprocal_sqrt, scale=1.0 / D, bias=EPS)
+            back = psum.tile([P, P], F32, name=f"back{pair}")
+            nc.tensor.transpose(back[:], rstd_turned[:], identity[:])
+            return back[:].rearrange("p (g t) -> p g t", t=PACK)
 
-        def gain(u):
-            factor[u] = keep.tile([P, GROUPS, PACK], F32, name=f"factor{u}")
-            nc.vector.tensor_tensor(out=factor[u][:], in0=rstd[u][:],
-                                    in1=gam_sb[:].unsqueeze(1).broadcast_to([P, GROUPS, PACK]), op=ALU.mult)
+        def gain(name, values):
+            scaled = keep.tile(list(values.shape), F32, name=name)
+            nc.vector.tensor_tensor(out=scaled[:], in0=values, in1=gam_sb[:].unsqueeze(1).broadcast_to(list(values.shape)), op=ALU.mult)
+            return scaled
 
-        def normalise(u):
-            z[u] = keep.tile(full, BF16, name=f"z{u}", align_bytes=64)
-            nc.vector.tensor_tensor(out=z[u][:], in0=dd[u][:], in1=factor[u][:].unsqueeze(2).broadcast_to(full), op=ALU.mult)
+        def normalise(values, factor, z):
+            nc.vector.tensor_tensor(out=z.rearrange("p (v d) t -> p v d t", d=D), in0=values,
+                                    in1=factor.unsqueeze(2).broadcast_to(full), op=ALU.mult)
 
-        def second_layer(u):
-            z_codes = keep.tile([P, CHUNK], U32, name=f"z_codes{u}", align_bytes=64)
-            z_sc = keep.tile([P, CHUNK], U8, name=f"z_sc{u}", align_bytes=64)
-            nc.vector.quantize_mx(out=z_codes[:].bitcast(FP8X4), scales=z_sc[:], in_=z[u][:].rearrange("p v d t -> p (v d t)"))
-            acc = psum.tile([P, N // P, CHUNK], F32, name=f"acc{u}")
+        def quantise(name, z):
+            width = z.shape[1]
+            z_codes = keep.tile([P, width], U32, name=f"{name}_codes", align_bytes=64)
+            z_sc = keep.tile([P, width], U8, name=f"{name}_sc", align_bytes=64)
+            nc.vector.quantize_mx(out=z_codes[:].bitcast(FP8X4), scales=z_sc[:], in_=z.rearrange("p c t -> p (c t)"))
+            return z_codes, z_sc
+
+        def product(acc, h, z_codes, z_sc):
+            nc.tensor.matmul_mx(
+                out=acc,
+                lhsT=w2_codes[:, h * P : (h + 1) * P].bitcast(FP8X4),
+                lhsT_scale=w2_sc[:, h * P : (h + 1) * P],
+                rhs=z_codes[:].bitcast(FP8X4),
+                rhs_scale=z_sc[:],
+                start=True, stop=True,
+            )
+
+        def second_layer(first, tag, z_codes, z_sc):
+            width = z_codes.shape[1]
+            acc = psum.tile([P, N // P, width], F32, name=f"acc{first}", tag=tag)
             for h in range(N // P):
-                nc.tensor.matmul_mx(
-                    out=acc[:, h, :],
-                    lhsT=w2_codes[:, h * P : (h + 1) * P].bitcast(FP8X4),
-                    lhsT_scale=w2_sc[:, h * P : (h + 1) * P],
-                    rhs=z_codes[:].bitcast(FP8X4),
-                    rhs_scale=z_sc[:],
-                    start=True, stop=True,
-                )
-            res = keep.tile([P, N // P, CHUNK], F32, name=f"res{u}")
+                product(acc[:, h, :], h, z_codes, z_sc)
+            res = keep.tile([P, N // P, width], F32, name=f"res{first}")
             nc.scalar.activation(out=res[:], in_=acc[:], func=ACT.Relu)
-            nc.sync.dma_start(out=out.rearrange("(h p) j -> p h j", p=P)[:, :, u * CHUNK : (u + 1) * CHUNK], in_=res[:])
+            nc.sync.dma_start(out=out.rearrange("(h p) j -> p h j", p=P)[:, :, first : first + width], in_=res[:])
 
-        for step in range(CHUNKS + 4):
-            if step < CHUNKS:
-                group_mean(step)
-            if 1 <= step < CHUNKS + 1:
-                center(step - 1)
-            if step in (1, 2):
-                w2_cast(step - 1)
-            if 2 <= step < CHUNKS + 2:
-                deviation(step - 2)
-            if step == 3:
-                w2_quantize()
-            if 3 <= step < CHUNKS + 3:
-                gain(step - 3)
-            if 4 <= step:
-                second_layer(step - 4)
-            if 3 <= step < CHUNKS + 3:
-                normalise(step - 3)
+        z_early = keep.tile([P, HALF, PACK], BF16, name="z_early", align_bytes=64)
+        for u in (2, 3):
+            z_bf[u] = keep.tile([P, CHUNK, PACK], BF16, name=f"z{u}", align_bytes=64)
+
+        group_mean(0)
+        w2_bf = keep.tile([P, N, PACK], BF16, name="w2_bf", tag="total0", align_bytes=64)
+        nc.gpsimd.tensor_scalar(out=w2_bf[:], in0=w2_raw[:].rearrange("p j c -> p c j"),
+                                scalar1=1.0, scalar2=0.0, op0=ALU.mult, op1=ALU.add)
+        group_mean(1)
+        center(0)
+        rstd_early = deviation(0)
+        group_mean(2)
+        group_mean(3)
+        center(1)
+        rstd_late = deviation(1)
+        factor_early = gain("factor_early", rstd_early)
+        nc.vector.quantize_mx(out=w2_codes[:].bitcast(FP8X4), scales=w2_sc[:], in_=w2_bf[:].rearrange("p c j -> p (c j)"))
+        normalise(dd[0][:], factor_early[:, :GROUPS], z_early[:, :CHUNK, :])
+        normalise(dd[1][:], factor_early[:, GROUPS:], z_early[:, CHUNK:, :])
+        dd_gained = gain("dd_gained", dd[2][:].rearrange("p v d t -> p (v d) t"))
+        second_layer(0, "turned1", *quantise("z_early", z_early[:]))
+        factor_last = gain("factor_last", rstd_late[:, GROUPS:])
+        normalise(dd_gained[:].rearrange("p (v d) t -> p v d t", d=D), rstd_late[:, :GROUPS], z_bf[2][:])
+        normalise(dd[3][:], factor_last[:], z_bf[3][:])
+        second_layer(2 * CHUNK, "bank2", *quantise("z2", z_bf[2][:]))
+
+        last = slice(3 * CHUNK, S)
+        z_codes, z_sc = quantise("z3", z_bf[3][:])
+        acc_low = psum.tile([P, CHUNK], F32, name="acc_low", tag="bank3")
+        acc_high = psum.tile([P, CHUNK], F32, name="acc_high", tag="bank1")
+        product(acc_low[:], 0, z_codes, z_sc)
+        product(acc_high[:], 1, z_codes, z_sc)
+        res_low = keep.tile([P, CHUNK], F32, name="res_low")
+        res_high = keep.tile([P, CHUNK], F32, name="res_high")
+        nc.scalar.activation(out=res_low[:], in_=acc_low[:], func=ACT.Relu)
+        nc.scalar.dma_start(out=out[:P, last], in_=res_low[:])
+        nc.vector.tensor_relu(out=res_high[:], in_=acc_high[:])
+        nc.sync.dma_start(out=out[P:, last], in_=res_high[:])

@@ -41,11 +41,13 @@ def tile_picked_ygrp_relu_p_kernel(tc, x_words, x_scales, w1, w2, gam, offs, out
         gam_sb = keep.tile([P, PACK], F32, name="gam_sb")
 
         nc.gpsimd.memset(table_scales[:].bitcast(I32), 0)
-        nc.sync.dma_start(out=w1_raw[:], in_=w1.rearrange("(p j) c -> p j c", j=PACK))
+        w1_rows = w1.rearrange("(p j) c -> p j c", j=PACK)
+        nc.sync.dma_start(out=w1_raw[:, :2], in_=w1_rows[:, :2])
         nc.sync.dma_start(offsets[:], offs)
         for q in range(4):
             nc.sync.dma_start(out=table_scales[32 * q : 32 * q + 4, :].bitcast(I32),
                               in_=x_scales[0, 4 * q : 4 * q + 4, :].bitcast(I32))
+        nc.sync.dma_start(out=w1_raw[:, 2:], in_=w1_rows[:, 2:])
         nc.sync.dma_start(out=table_words[:].bitcast(I32), in_=x_words[0].rearrange("p c r -> p (c r)").bitcast(I32))
         nc.sync.dma_start(out=w2_raw[:], in_=w2.rearrange("(p j) c -> p j c", j=PACK))
         nc.sync.dma_start(out=gam_sb[:], in_=gam.rearrange("(p t) o -> p (t o)", t=PACK))
@@ -58,6 +60,9 @@ def tile_picked_ygrp_relu_p_kernel(tc, x_words, x_scales, w1, w2, gam, offs, out
         nc.vector.memset(warm_in[:], 1.0)
         nc.scalar.activation(out=warm_out[:], in_=warm_in[:], func=ACT.Abs_reciprocal_sqrt)
 
+        x_sc = keep.tile([P, S], U8, name="x_sc", align_bytes=64)
+        nc.vector.tensor_copy(x_sc[:], table_scales[:].indirect(offsets[:]))
+
         w1_bf = keep.tile([P, PACK * P * PACK], BF16, name="w1_bf", align_bytes=64)
         w1_dst = w1_bf[:].rearrange("p (t m j) -> p m t j", t=PACK, j=PACK)
         w1_src = w1_raw[:].rearrange("p j (m t) -> p m t j", t=PACK)
@@ -67,9 +72,6 @@ def tile_picked_ygrp_relu_p_kernel(tc, x_words, x_scales, w1, w2, gam, offs, out
         w1_codes = keep.tile([P, H], U32, name="w1_codes", align_bytes=64)
         w1_sc = keep.tile([P, H], U8, name="w1_sc", align_bytes=64)
         nc.vector.quantize_mx(out=w1_codes[:].bitcast(FP8X4), scales=w1_sc[:], in_=w1_bf[:])
-
-        x_sc = keep.tile([P, S], U8, name="x_sc", align_bytes=64)
-        nc.vector.tensor_copy(x_sc[:], table_scales[:].indirect(offsets[:]))
 
         x_codes = []
         for h in range(2):

@@ -35,21 +35,17 @@ def tile_picked_ygrp_relu_p_kernel(tc, x_words, x_scales, w1, w2, gam, offs, out
 
         offsets = keep.tile([P, S // 16], U16, name="offsets")
         table_words = keep.tile([P, T], U32, name="table_words", align_bytes=64)
-        table_scales = keep.tile([P, T], U8, name="table_scales", align_bytes=64)
+        table_scales = keep.tile([P, T], U8, name="table_scales", tag="scales_then_w2", align_bytes=64)
         w1_raw = keep.tile([P, PACK, H], F32, name="w1_raw", align_bytes=64)
-        w2_raw = keep.tile([P, PACK, N], F32, name="w2_raw", align_bytes=64)
         gam_sb = keep.tile([P, PACK], F32, name="gam_sb")
 
         nc.gpsimd.memset(table_scales[:].bitcast(I32), 0)
         w1_rows = w1.rearrange("(p j) c -> p j c", j=PACK)
         nc.sync.dma_start(out=w1_raw[:, :2], in_=w1_rows[:, :2])
         nc.sync.dma_start(offsets[:], offs)
-        for q in range(4):
-            nc.sync.dma_start(out=table_scales[32 * q : 32 * q + 4, :].bitcast(I32),
-                              in_=x_scales[0, 4 * q : 4 * q + 4, :].bitcast(I32))
+        nc.sync.dma_start(out=table_scales[0:P:8, :].bitcast(I32), in_=x_scales[0].bitcast(I32))
         nc.sync.dma_start(out=w1_raw[:, 2:], in_=w1_rows[:, 2:])
         nc.sync.dma_start(out=table_words[:].bitcast(I32), in_=x_words[0].rearrange("p c r -> p (c r)").bitcast(I32))
-        nc.sync.dma_start(out=w2_raw[:], in_=w2.rearrange("(p j) c -> p j c", j=PACK))
         nc.sync.dma_start(out=gam_sb[:], in_=gam.rearrange("(p t) o -> p (t o)", t=PACK))
 
         identity = keep.tile([P, P], F32, name="identity")
@@ -60,8 +56,14 @@ def tile_picked_ygrp_relu_p_kernel(tc, x_words, x_scales, w1, w2, gam, offs, out
         nc.vector.memset(warm_in[:], 1.0)
         nc.scalar.activation(out=warm_out[:], in_=warm_in[:], func=ACT.Abs_reciprocal_sqrt)
 
+        x_spread = keep.tile([P, S], U8, name="x_spread", align_bytes=64)
         x_sc = keep.tile([P, S], U8, name="x_sc", align_bytes=64)
-        nc.vector.tensor_copy(x_sc[:], table_scales[:].indirect(offsets[:]))
+        nc.gpsimd.memset(x_sc[:].bitcast(I32), 0)
+        nc.vector.tensor_copy(x_spread[:], table_scales[:].indirect(offsets[:]))
+        for q in range(4):
+            nc.sync.dma_start(out=x_sc[32 * q : 32 * q + 4, :].bitcast(I32), in_=x_spread[32 * q : 32 * q + 32 : 8, :].bitcast(I32))
+        w2_raw = keep.tile([P, PACK, N], F32, name="w2_raw", tag="scales_then_w2", align_bytes=64)
+        nc.sync.dma_start(out=w2_raw[:], in_=w2.rearrange("(p j) c -> p j c", j=PACK))
 
         w1_bf = keep.tile([P, PACK * P * PACK], BF16, name="w1_bf", align_bytes=64)
         w1_dst = w1_bf[:].rearrange("p (t m j) -> p m t j", t=PACK, j=PACK)
@@ -135,7 +137,7 @@ def tile_picked_ygrp_relu_p_kernel(tc, x_words, x_scales, w1, w2, gam, offs, out
 
         def normalise(values, factor, z):
             nc.vector.tensor_tensor(out=z.rearrange("p (v d) t -> p v d t", d=D), in0=values,
-                                    in1=factor.unsqueeze(2).broadcast_to(full), op=ALU.mult)
+                                    in1=factor.unsqueeze(2).broadcast_to(list(values.shape)), op=ALU.mult)
 
         def quantise(name, z):
             width = z.shape[1]
@@ -164,8 +166,7 @@ def tile_picked_ygrp_relu_p_kernel(tc, x_words, x_scales, w1, w2, gam, offs, out
             nc.sync.dma_start(out=out.rearrange("(h p) j -> p h j", p=P)[:, :, first : first + width], in_=res[:])
 
         z_early = keep.tile([P, HALF, PACK], BF16, name="z_early", align_bytes=64)
-        for u in (2, 3):
-            z_bf[u] = keep.tile([P, CHUNK, PACK], BF16, name=f"z{u}", align_bytes=64)
+        z_bf[2] = keep.tile([P, CHUNK, PACK], BF16, name="z2", align_bytes=64)
 
         group_mean(0)
         w2_bf = keep.tile([P, N, PACK], BF16, name="w2_bf", tag="total0", align_bytes=64)
@@ -186,11 +187,17 @@ def tile_picked_ygrp_relu_p_kernel(tc, x_words, x_scales, w1, w2, gam, offs, out
         second_layer(0, "turned1", *quantise("z_early", z_early[:]))
         factor_last = gain("factor_last", rstd_late[:, GROUPS:])
         normalise(dd_gained[:].rearrange("p (v d) t -> p v d t", d=D), rstd_late[:, :GROUPS], z_bf[2][:])
-        normalise(dd[3][:], factor_last[:], z_bf[3][:])
+        z_last = [keep.tile([P, CHUNK // 2, PACK], BF16, name=f"z_last{h}", align_bytes=64) for h in range(2)]
+        z_codes = keep.tile([P, CHUNK], U32, name="z_last_codes", align_bytes=64)
+        z_sc = keep.tile([P, CHUNK], U8, name="z_last_sc", align_bytes=64)
+        normalise(dd[3][:, : GROUPS // 2], factor_last[:, : GROUPS // 2], z_last[0][:])
         second_layer(2 * CHUNK, "bank2", *quantise("z2", z_bf[2][:]))
+        normalise(dd[3][:, GROUPS // 2 :], factor_last[:, GROUPS // 2 :], z_last[1][:])
+        for h in range(2):
+            cols = slice(h * CHUNK // 2, (h + 1) * CHUNK // 2)
+            nc.vector.quantize_mx(out=z_codes[:, cols].bitcast(FP8X4), scales=z_sc[:, cols], in_=z_last[h][:].rearrange("p c t -> p (c t)"))
 
         last = slice(3 * CHUNK, S)
-        z_codes, z_sc = quantise("z3", z_bf[3][:])
         acc_low = psum.tile([P, CHUNK], F32, name="acc_low", tag="bank3")
         acc_high = psum.tile([P, CHUNK], F32, name="acc_high", tag="bank1")
         product(acc_low[:], 0, z_codes, z_sc)

@@ -99,45 +99,35 @@ def tile_picked_ygrp_relu_p_kernel(tc, x_words, x_scales, w1, w2, gam, offs, out
         w2_codes = keep.tile([P, N], U32, name="w2_codes", align_bytes=64)
         w2_sc = keep.tile([P, N], U8, name="w2_sc", align_bytes=64)
 
-        full = [P, GROUPS, D, PACK]
-        mean, z_bf = {}, {}
-        dd = [keep.tile(full, F32, name=f"dd{u}") for u in range(CHUNKS)]
-        ee = {}
+        WIDE = GROUPS * PACK
+        total, ee, gained = {}, {}, {}
 
-        def group_mean(u):
-            total = keep.tile([P, GROUPS, PACK], F32, name=f"total{u}", tag=(f"stat{u - 2}" if u >= 2 else f"total{u}"), align_bytes=64)
-            nc.vector.tensor_reduce(out=total[:], in_=y[u][:].rearrange("p t (v d) -> p v t d", d=D), axis=AX.X, op=ALU.add)
-            mean[u] = keep.tile([P, GROUPS, PACK], F32, name=f"mean{u}", tag=(f"stat{u}" if u < 2 else f"mean{u}"), align_bytes=64)
-            nc.scalar.activation(out=mean[u][:], in_=total[:], func=ACT.Copy, scale=1.0 / D)
+        def group_sum(u, tag):
+            total[u] = keep.tile([P, WIDE], F32, name=f"total{u}", tag=tag, align_bytes=64)
+            nc.vector.tensor_reduce(out=total[u][:], in_=y[u][:].rearrange("p t (v d) -> p (t v) d", d=D), axis=AX.X, op=ALU.add)
 
-        def center(pair):
-            half = [P, GROUPS, D // 2, PACK]
-            for h in range(2):
-                ee[pair, h] = keep.tile([P, D // 2, 2, GROUPS, PACK], F32, name=f"ee{pair}_{h}", tag=f"ee{(pair + h) % 2}")
-                for u in (2 * pair, 2 * pair + 1):
-                    members = y[u][:].rearrange("p t (v h d) -> p h v d t", h=2, d=D // 2)[:, h]
-                    nc.vector.tensor_tensor(out=dd[u][:, :, h * D // 2 : (h + 1) * D // 2], in0=members, in1=mean[u][:].unsqueeze(2).broadcast_to(half), op=ALU.subtract)
-                    nc.scalar.activation(out=ee[pair, h][:, :, u % 2].rearrange("p d v t -> p v d t"), in_=dd[u][:, :, h * D // 2 : (h + 1) * D // 2], func=ACT.Square)
+        def center(u, ds, squares):
+            count = ds.stop - ds.start
+            nc.vector.scalar_tensor_tensor(out=dd[u][:, ds], in0=total[u][:].unsqueeze(1).broadcast_to([P, count, WIDE]), scalar=-1.0 / D,
+                                           in1=y[u][:].rearrange("p t (v d) -> p d (t v)", d=D)[:, ds], op0=ALU.mult, op1=ALU.add)
+            nc.scalar.activation(out=squares, in_=dd[u][:, ds], func=ACT.Square)
+            nc.gpsimd.tensor_tensor(out=gained[u][:, ds], in0=dd[u][:, ds].rearrange("p d (t v) -> p d v t", t=PACK),
+                                    in1=gam_sb[:].unsqueeze(1).unsqueeze(1).broadcast_to([P, count, GROUPS, PACK]), op=ALU.mult)
 
-        def deviation(pair):
-            turned = psum.tile([P, P], F32, name=f"turned{pair}", tag=f"turned{pair}")
+        def deviation(name, columns):
+            turned = psum.tile([P, P], F32, name=f"turned{name}", tag=f"turned{name}")
             for d in range(D):
-                nc.tensor.matmul(out=turned[:], lhsT=ee[pair, d // 4][:, d % 4].rearrange("p u v t -> p (u v t)"), rhs=identity[:],
-                                 is_transpose=True, start=(d == 0), stop=(d == D - 1))
-            rstd_turned = keep.tile([P, P], F32, name=f"rstd_turned{pair}")
+                nc.tensor.matmul(out=turned[:], lhsT=columns(d), rhs=identity[:], is_transpose=True, start=(d == 0), stop=(d == D - 1))
+            rstd_turned = keep.tile([P, P], F32, name=f"rstd_turned{name}")
             nc.scalar.activation(out=rstd_turned[:], in_=turned[:], func=ACT.Abs_reciprocal_sqrt, scale=1.0 / D, bias=EPS)
-            back = psum.tile([P, P], F32, name=f"back{pair}")
+            back = psum.tile([P, P], F32, name=f"back{name}")
             nc.tensor.transpose(back[:], rstd_turned[:], identity[:])
-            return back[:].rearrange("p (g t) -> p g t", t=PACK)
+            return back[:]
 
-        def gain(name, values):
-            scaled = keep.tile(list(values.shape), F32, name=name)
-            nc.vector.tensor_tensor(out=scaled[:], in0=values, in1=gam_sb[:].unsqueeze(1).broadcast_to(list(values.shape)), op=ALU.mult)
-            return scaled
-
-        def normalise(values, factor, z):
-            nc.vector.tensor_tensor(out=z.rearrange("p (v d) t -> p v d t", d=D), in0=values,
-                                    in1=factor.unsqueeze(2).broadcast_to(list(values.shape)), op=ALU.mult)
+        def normalise(values, rstd, z):
+            count = values.shape[1]
+            nc.vector.tensor_tensor(out=z.rearrange("p (d v) t -> p d v t", v=GROUPS), in0=values,
+                                    in1=rstd.rearrange("p (t v) -> p v t", t=PACK).unsqueeze(1).broadcast_to([P, count, GROUPS, PACK]), op=ALU.mult)
 
         def quantise(name, z):
             width = z.shape[1]
@@ -156,55 +146,83 @@ def tile_picked_ygrp_relu_p_kernel(tc, x_words, x_scales, w1, w2, gam, offs, out
                 start=True, stop=True,
             )
 
-        def second_layer(first, tag, z_codes, z_sc):
+        def second_layer(first, tag, order, z_codes, z_sc):
             width = z_codes.shape[1]
             acc = psum.tile([P, N // P, width], F32, name=f"acc{first}", tag=tag)
             for h in range(N // P):
                 product(acc[:, h, :], h, z_codes, z_sc)
             res = keep.tile([P, N // P, width], F32, name=f"res{first}")
-            nc.scalar.activation(out=res[:], in_=acc[:], func=ACT.Relu)
+            nc.scalar.activation(out=res[:].rearrange("p h (u v d) -> p (h u) v d", v=GROUPS, d=D),
+                                 in_=acc[:].rearrange(f"p h {order} -> p (h u) v d", v=GROUPS, d=D), func=ACT.Relu)
             nc.sync.dma_start(out=out.rearrange("(h p) j -> p h j", p=P)[:, :, first : first + width], in_=res[:])
 
-        z_early = keep.tile([P, HALF, PACK], BF16, name="z_early", align_bytes=64)
-        z_bf[2] = keep.tile([P, CHUNK, PACK], BF16, name="z2", align_bytes=64)
+        def last_layer(first, z_codes, z_sc, tag_low, tag_high):
+            last = slice(first, first + CHUNK)
+            acc_low = psum.tile([P, CHUNK], F32, name="acc_low", tag=tag_low)
+            acc_high = psum.tile([P, CHUNK], F32, name="acc_high", tag=tag_high)
+            product(acc_low[:], 0, z_codes, z_sc)
+            product(acc_high[:], 1, z_codes, z_sc)
+            res_low = keep.tile([P, CHUNK], F32, name="res_low")
+            res_high = keep.tile([P, CHUNK], F32, name="res_high")
+            nc.scalar.activation(out=res_low[:].rearrange("p (v d) -> p v d", d=D), in_=acc_low[:].rearrange("p (d v) -> p v d", d=D), func=ACT.Relu)
+            nc.scalar.dma_start(out=out[:P, last], in_=res_low[:])
+            nc.vector.tensor_relu(out=res_high[:].rearrange("p (v d) -> p v d", d=D), in_=acc_high[:].rearrange("p (d v) -> p v d", d=D))
+            nc.sync.dma_start(out=out[P:, last], in_=res_high[:])
 
-        group_mean(0)
-        w2_bf = keep.tile([P, N, PACK], BF16, name="w2_bf", tag="total0", align_bytes=64)
-        nc.gpsimd.tensor_scalar(out=w2_bf[:], in0=w2_raw[:].rearrange("p j c -> p c j"),
-                                scalar1=1.0, scalar2=0.0, op0=ALU.mult, op1=ALU.add)
-        group_mean(1)
-        center(0)
-        rstd_early = deviation(0)
-        group_mean(2)
-        group_mean(3)
-        center(1)
-        rstd_late = deviation(1)
-        factor_early = gain("factor_early", rstd_early)
+
+        turned_chunks = (0, 1, 3)
+        dd = {u: keep.tile([P, D, WIDE], F32, name=f"dd{u}") for u in turned_chunks}
+        for u in turned_chunks:
+            gained[u] = keep.tile([P, D, GROUPS, PACK], F32, name=f"gained{u}")
+        halves = [slice(0, D // 2), slice(D // 2, D)]
+        ee_early = [keep.tile([P, D // 2, 2, WIDE], F32, name=f"ee_early{h}") for h in range(2)]
+        ee3 = keep.tile([P, D + 1, WIDE], F32, name="ee3")
+        nc.gpsimd.memset(ee3[:, 0], 0.0)
+
+        w2_bf = keep.tile([P, N, PACK], BF16, name="w2_bf", align_bytes=64)
+        nc.scalar.copy(out=w2_bf[:], in_=w2_raw[:].rearrange("p j c -> p c j"))
+
+        group_sum(0, "total0")
+        group_sum(1, "total1")
+        for h in range(2):
+            for u in range(2):
+                center(u, halves[h], ee_early[h][:, :, u])
+        rstd_early = deviation(0, lambda d: ee_early[d // 4][:, d % 4].rearrange("p u w -> p (u w)"))
+        group_sum(2, "total2")
+        group_sum(3, "total3")
+
+        dd2 = keep.tile([P, WIDE, D], F32, name="dd2")
+        ee2 = keep.tile([P, WIDE, D], F32, name="ee2")
+        nc.vector.scalar_tensor_tensor(out=dd2[:], in0=total[2][:].unsqueeze(2).broadcast_to([P, WIDE, D]), scalar=-1.0 / D,
+                                       in1=y[2][:].rearrange("p t (v d) -> p (t v) d", d=D), op0=ALU.mult, op1=ALU.add)
+        nc.scalar.activation(out=ee2[:], in_=dd2[:], func=ACT.Square)
+        for ds in (slice(0, 2), slice(2, 5), slice(5, D)):
+            center(3, ds, ee3[:, ds.start + 1 : ds.stop + 1])
+        rstd3 = deviation(3, lambda d: ee3[:, d : d + 2].rearrange("p d w -> p (d w)"))[:, WIDE:]
+
         nc.vector.quantize_mx(out=w2_codes[:].bitcast(FP8X4), scales=w2_sc[:], in_=w2_bf[:].rearrange("p c j -> p (c j)"))
-        normalise(dd[0][:], factor_early[:, :GROUPS], z_early[:, :CHUNK, :])
-        normalise(dd[1][:], factor_early[:, GROUPS:], z_early[:, CHUNK:, :])
-        dd_gained = gain("dd_gained", dd[2][:].rearrange("p v d t -> p (v d) t"))
-        second_layer(0, "turned1", *quantise("z_early", z_early[:]))
-        factor_last = gain("factor_last", rstd_late[:, GROUPS:])
-        normalise(dd_gained[:].rearrange("p (v d) t -> p v d t", d=D), rstd_late[:, :GROUPS], z_bf[2][:])
+        var2 = keep.tile([P, WIDE], F32, name="var2")
+        nc.vector.tensor_reduce(out=var2[:], in_=ee2[:], axis=AX.X, op=ALU.add)
+        rstd2 = keep.tile([P, WIDE], F32, name="rstd2")
+        nc.scalar.activation(out=rstd2[:], in_=var2[:], func=ACT.Abs_reciprocal_sqrt, scale=1.0 / D, bias=EPS)
+
+        z_early = keep.tile([P, HALF, PACK], BF16, name="z_early", align_bytes=64)
+        normalise(gained[0][:], rstd_early[:, :WIDE], z_early[:, :CHUNK, :])
+        normalise(gained[1][:], rstd_early[:, WIDE:], z_early[:, CHUNK:, :])
+        factor2 = keep.tile([P, GROUPS, PACK], F32, name="factor2")
+        nc.vector.tensor_tensor(out=factor2[:], in0=rstd2[:].rearrange("p (t v) -> p v t", t=PACK),
+                                in1=gam_sb[:].unsqueeze(1).broadcast_to([P, GROUPS, PACK]), op=ALU.mult)
+        second_layer(0, "bank0", "(u d v)", *quantise("z_early", z_early[:]))
+        z2 = keep.tile([P, CHUNK, PACK], BF16, name="z2", align_bytes=64)
+        nc.vector.tensor_tensor(out=z2[:].rearrange("p (v d) t -> p v d t", d=D), in0=dd2[:].rearrange("p (t v) d -> p v d t", t=PACK),
+                                in1=factor2[:].unsqueeze(2).broadcast_to([P, GROUPS, D, PACK]), op=ALU.mult)
         z_last = [keep.tile([P, CHUNK // 2, PACK], BF16, name=f"z_last{h}", align_bytes=64) for h in range(2)]
         z_codes = keep.tile([P, CHUNK], U32, name="z_last_codes", align_bytes=64)
         z_sc = keep.tile([P, CHUNK], U8, name="z_last_sc", align_bytes=64)
-        normalise(dd[3][:, : GROUPS // 2], factor_last[:, : GROUPS // 2], z_last[0][:])
-        second_layer(2 * CHUNK, "bank2", *quantise("z2", z_bf[2][:]))
-        normalise(dd[3][:, GROUPS // 2 :], factor_last[:, GROUPS // 2 :], z_last[1][:])
+        normalise(gained[3][:, halves[0]], rstd3, z_last[0][:])
+        second_layer(2 * CHUNK, "bank2", "(u v d)", *quantise("z2", z2[:]))
+        normalise(gained[3][:, halves[1]], rstd3, z_last[1][:])
         for h in range(2):
             cols = slice(h * CHUNK // 2, (h + 1) * CHUNK // 2)
             nc.vector.quantize_mx(out=z_codes[:, cols].bitcast(FP8X4), scales=z_sc[:, cols], in_=z_last[h][:].rearrange("p c t -> p (c t)"))
-
-        last = slice(3 * CHUNK, S)
-        acc_low = psum.tile([P, CHUNK], F32, name="acc_low", tag="bank3")
-        acc_high = psum.tile([P, CHUNK], F32, name="acc_high", tag="bank1")
-        product(acc_low[:], 0, z_codes, z_sc)
-        product(acc_high[:], 1, z_codes, z_sc)
-        res_low = keep.tile([P, CHUNK], F32, name="res_low")
-        res_high = keep.tile([P, CHUNK], F32, name="res_high")
-        nc.scalar.activation(out=res_low[:], in_=acc_low[:], func=ACT.Relu)
-        nc.scalar.dma_start(out=out[:P, last], in_=res_low[:])
-        nc.vector.tensor_relu(out=res_high[:], in_=acc_high[:])
-        nc.sync.dma_start(out=out[P:, last], in_=res_high[:])
+        last_layer(3 * CHUNK, z_codes, z_sc, "bank3", "bank1")

@@ -43,7 +43,8 @@ def tile_picked_ygrp_relu_p_kernel(tc, x_words, x_scales, w1, w2, gam, offs, out
         w1_rows = w1.rearrange("(p j) c -> p j c", j=PACK)
         nc.sync.dma_start(out=w1_raw[:, :2], in_=w1_rows[:, :2])
         nc.sync.dma_start(offsets[:], offs)
-        nc.sync.dma_start(out=table_scales[0:P:8, :].bitcast(I32), in_=x_scales[0].bitcast(I32))
+        for q in range(4):
+            nc.sync.dma_start(out=table_scales[32 * q : 32 * q + 4, :].bitcast(I32), in_=x_scales[0, 4 * q : 4 * q + 4].bitcast(I32))
         nc.sync.dma_start(out=w1_raw[:, 2:], in_=w1_rows[:, 2:])
         nc.sync.dma_start(out=table_words[:].bitcast(I32), in_=x_words[0].rearrange("p c r -> p (c r)").bitcast(I32))
         nc.sync.dma_start(out=gam_sb[:], in_=gam.rearrange("(p t) o -> p (t o)", t=PACK))
@@ -56,12 +57,8 @@ def tile_picked_ygrp_relu_p_kernel(tc, x_words, x_scales, w1, w2, gam, offs, out
         nc.vector.memset(warm_in[:], 1.0)
         nc.scalar.activation(out=warm_out[:], in_=warm_in[:], func=ACT.Abs_reciprocal_sqrt)
 
-        x_spread = keep.tile([P, S], U8, name="x_spread", align_bytes=64)
         x_sc = keep.tile([P, S], U8, name="x_sc", align_bytes=64)
-        nc.gpsimd.memset(x_sc[:].bitcast(I32), 0)
-        nc.vector.tensor_copy(x_spread[:], table_scales[:].indirect(offsets[:]))
-        for q in range(4):
-            nc.sync.dma_start(out=x_sc[32 * q : 32 * q + 4, :].bitcast(I32), in_=x_spread[32 * q : 32 * q + 32 : 8, :].bitcast(I32))
+        nc.vector.tensor_copy(x_sc[:], table_scales[:].indirect(offsets[:]))
         w2_raw = keep.tile([P, PACK, N], F32, name="w2_raw", tag="scales_then_w2", align_bytes=64)
         nc.sync.dma_start(out=w2_raw[:], in_=w2.rearrange("(p j) c -> p j c", j=PACK))
 
@@ -83,18 +80,19 @@ def tile_picked_ygrp_relu_p_kernel(tc, x_words, x_scales, w1, w2, gam, offs, out
 
         y = []
         for u in range(CHUNKS):
-            bank = psum.tile([P, PACK, CHUNK], F32, name=f"y{u}", tag=f"bank{u}")
+            slots = PACK // 2 if u == 0 else PACK
+            banks = [psum.tile([P, slots, CHUNK], F32, name=f"y{u}_{b}", tag=f"bank{u}_{b}") for b in range(PACK // slots)]
             c0 = u * CHUNK % HALF
             for t in range(PACK):
                 nc.tensor.matmul_mx(
-                    out=bank[:, t, :],
+                    out=banks[t // slots][:, t % slots, :],
                     lhsT=w1_codes[:, t * P : (t + 1) * P].bitcast(FP8X4),
                     lhsT_scale=w1_sc[:, t * P : (t + 1) * P],
                     rhs=x_codes[u * CHUNK // HALF][:, c0 : c0 + CHUNK].bitcast(FP8X4),
                     rhs_scale=x_sc[:, u * CHUNK : (u + 1) * CHUNK],
                     start=True, stop=True,
                 )
-            y.append(bank)
+            y.append(banks if u == 0 else banks[0])
 
         w2_codes = keep.tile([P, N], U32, name="w2_codes", align_bytes=64)
         w2_sc = keep.tile([P, N], U8, name="w2_sc", align_bytes=64)
@@ -110,9 +108,21 @@ def tile_picked_ygrp_relu_p_kernel(tc, x_words, x_scales, w1, w2, gam, offs, out
             count = ds.stop - ds.start
             nc.vector.scalar_tensor_tensor(out=dd[u][:, ds], in0=total[u][:].unsqueeze(1).broadcast_to([P, count, WIDE]), scalar=-1.0 / D,
                                            in1=y[u][:].rearrange("p t (v d) -> p d (t v)", d=D)[:, ds], op0=ALU.mult, op1=ALU.add)
+            square_and_gain(u, ds, squares)
+
+        def square_and_gain(u, ds, squares):
+            count = ds.stop - ds.start
             nc.scalar.activation(out=squares, in_=dd[u][:, ds], func=ACT.Square)
             nc.gpsimd.tensor_tensor(out=gained[u][:, ds], in0=dd[u][:, ds].rearrange("p d (t v) -> p d v t", t=PACK),
                                     in1=gam_sb[:].unsqueeze(1).unsqueeze(1).broadcast_to([P, count, GROUPS, PACK]), op=ALU.mult)
+
+        def first_sum(b):
+            nc.vector.tensor_reduce(out=total[0][:, b * WIDE // 2 : (b + 1) * WIDE // 2], in_=y[0][b][:].rearrange("p t (v d) -> p (t v) d", d=D), axis=AX.X, op=ALU.add)
+
+        def first_center(b):
+            cols = slice(b * WIDE // 2, (b + 1) * WIDE // 2)
+            nc.vector.scalar_tensor_tensor(out=dd[0][:, :, cols], in0=total[0][:, cols].unsqueeze(1).broadcast_to([P, D, WIDE // 2]), scalar=-1.0 / D,
+                                           in1=y[0][b][:].rearrange("p t (v d) -> p d (t v)", d=D), op0=ALU.mult, op1=ALU.add)
 
         def deviation(name, columns):
             turned = psum.tile([P, P], F32, name=f"turned{name}", tag=f"turned{name}")
@@ -120,7 +130,7 @@ def tile_picked_ygrp_relu_p_kernel(tc, x_words, x_scales, w1, w2, gam, offs, out
                 nc.tensor.matmul(out=turned[:], lhsT=columns(d), rhs=identity[:], is_transpose=True, start=(d == 0), stop=(d == D - 1))
             rstd_turned = keep.tile([P, P], F32, name=f"rstd_turned{name}")
             nc.scalar.activation(out=rstd_turned[:], in_=turned[:], func=ACT.Abs_reciprocal_sqrt, scale=1.0 / D, bias=EPS)
-            back = psum.tile([P, P], F32, name=f"back{name}")
+            back = psum.tile([P, P], F32, name=f"back{name}", tag=f"turned{name}")
             nc.tensor.transpose(back[:], rstd_turned[:], identity[:])
             return back[:]
 
@@ -156,6 +166,15 @@ def tile_picked_ygrp_relu_p_kernel(tc, x_words, x_scales, w1, w2, gam, offs, out
                                  in_=acc[:].rearrange(f"p h {order} -> p (h u) v d", v=GROUPS, d=D), func=ACT.Relu)
             nc.sync.dma_start(out=out.rearrange("(h p) j -> p h j", p=P)[:, :, first : first + width], in_=res[:])
 
+        def early_layer(z_codes, z_sc):
+            for h in range(N // P):
+                acc = psum.tile([P, HALF], F32, name=f"acc_early{h}", tag=f"bank0_{h}")
+                product(acc[:], h, z_codes, z_sc)
+                res = keep.tile([P, HALF], F32, name=f"res_early{h}")
+                nc.scalar.activation(out=res[:].rearrange("p (u v d) -> p u v d", v=GROUPS, d=D),
+                                     in_=acc[:].rearrange("p (u d v) -> p u v d", v=GROUPS, d=D), func=ACT.Relu)
+                nc.sync.dma_start(out=out[h * P : (h + 1) * P, :HALF], in_=res[:])
+
         def last_layer(first, z_codes, z_sc, tag_low, tag_high):
             last = slice(first, first + CHUNK)
             acc_low = psum.tile([P, CHUNK], F32, name="acc_low", tag=tag_low)
@@ -182,11 +201,15 @@ def tile_picked_ygrp_relu_p_kernel(tc, x_words, x_scales, w1, w2, gam, offs, out
         w2_bf = keep.tile([P, N, PACK], BF16, name="w2_bf", align_bytes=64)
         nc.scalar.copy(out=w2_bf[:], in_=w2_raw[:].rearrange("p j c -> p c j"))
 
-        group_sum(0, "total0")
+        total[0] = keep.tile([P, WIDE], F32, name="total0", align_bytes=64)
+        first_sum(0)
+        first_sum(1)
+        first_center(0)
         group_sum(1, "total1")
+        first_center(1)
         for h in range(2):
-            for u in range(2):
-                center(u, halves[h], ee_early[h][:, :, u])
+            square_and_gain(0, halves[h], ee_early[h][:, :, 0])
+            center(1, halves[h], ee_early[h][:, :, 1])
         rstd_early = deviation(0, lambda d: ee_early[d // 4][:, d % 4].rearrange("p u w -> p (u w)"))
         group_sum(2, "total2")
         group_sum(3, "total3")
@@ -212,17 +235,17 @@ def tile_picked_ygrp_relu_p_kernel(tc, x_words, x_scales, w1, w2, gam, offs, out
         factor2 = keep.tile([P, GROUPS, PACK], F32, name="factor2")
         nc.vector.tensor_tensor(out=factor2[:], in0=rstd2[:].rearrange("p (t v) -> p v t", t=PACK),
                                 in1=gam_sb[:].unsqueeze(1).broadcast_to([P, GROUPS, PACK]), op=ALU.mult)
-        second_layer(0, "bank0", "(u d v)", *quantise("z_early", z_early[:]))
+        early_layer(*quantise("z_early", z_early[:]))
         z2 = keep.tile([P, CHUNK, PACK], BF16, name="z2", align_bytes=64)
         nc.vector.tensor_tensor(out=z2[:].rearrange("p (v d) t -> p v d t", d=D), in0=dd2[:].rearrange("p (t v) d -> p v d t", t=PACK),
                                 in1=factor2[:].unsqueeze(2).broadcast_to([P, GROUPS, D, PACK]), op=ALU.mult)
         z_last = [keep.tile([P, CHUNK // 2, PACK], BF16, name=f"z_last{h}", align_bytes=64) for h in range(2)]
         z_codes = keep.tile([P, CHUNK], U32, name="z_last_codes", align_bytes=64)
         z_sc = keep.tile([P, CHUNK], U8, name="z_last_sc", align_bytes=64)
+        second_layer(2 * CHUNK, "bank2_0", "(u v d)", *quantise("z2", z2[:]))
         normalise(gained[3][:, halves[0]], rstd3, z_last[0][:])
-        second_layer(2 * CHUNK, "bank2", "(u v d)", *quantise("z2", z2[:]))
         normalise(gained[3][:, halves[1]], rstd3, z_last[1][:])
         for h in range(2):
             cols = slice(h * CHUNK // 2, (h + 1) * CHUNK // 2)
             nc.vector.quantize_mx(out=z_codes[:, cols].bitcast(FP8X4), scales=z_sc[:, cols], in_=z_last[h][:].rearrange("p c t -> p (c t)"))
-        last_layer(3 * CHUNK, z_codes, z_sc, "bank3", "bank1")
+        last_layer(3 * CHUNK, z_codes, z_sc, "bank3_0", "bank1_0")

@@ -124,13 +124,13 @@ def tile_picked_ygrp_relu_p_kernel(tc, x_words, x_scales, w1, w2, gam, offs, out
             nc.vector.scalar_tensor_tensor(out=dd[0][:, :, cols], in0=total[0][:, cols].unsqueeze(1).broadcast_to([P, D, WIDE // 2]), scalar=-1.0 / D,
                                            in1=y[0][b][:].rearrange("p t (v d) -> p d (t v)", d=D), op0=ALU.mult, op1=ALU.add)
 
-        def deviation(name, columns):
+        def deviation(name, columns, back_tag):
             turned = psum.tile([P, P], F32, name=f"turned{name}", tag=f"turned{name}")
             for d in range(D):
                 nc.tensor.matmul(out=turned[:], lhsT=columns(d), rhs=identity[:], is_transpose=True, start=(d == 0), stop=(d == D - 1))
             rstd_turned = keep.tile([P, P], F32, name=f"rstd_turned{name}")
             nc.scalar.activation(out=rstd_turned[:], in_=turned[:], func=ACT.Abs_reciprocal_sqrt, scale=1.0 / D, bias=EPS)
-            back = psum.tile([P, P], F32, name=f"back{name}", tag=f"turned{name}")
+            back = psum.tile([P, P], F32, name=f"back{name}", tag=back_tag)
             nc.tensor.transpose(back[:], rstd_turned[:], identity[:])
             return back[:]
 
@@ -168,7 +168,7 @@ def tile_picked_ygrp_relu_p_kernel(tc, x_words, x_scales, w1, w2, gam, offs, out
 
         def early_layer(z_codes, z_sc):
             for h in range(N // P):
-                acc = psum.tile([P, HALF], F32, name=f"acc_early{h}", tag=f"bank0_{h}")
+                acc = psum.tile([P, HALF], F32, name=f"acc_early{h}", tag=("turned3", "bank0_1")[h])
                 product(acc[:], h, z_codes, z_sc)
                 res = keep.tile([P, HALF], F32, name=f"res_early{h}")
                 nc.scalar.activation(out=res[:].rearrange("p (u v d) -> p u v d", v=GROUPS, d=D),
@@ -210,7 +210,7 @@ def tile_picked_ygrp_relu_p_kernel(tc, x_words, x_scales, w1, w2, gam, offs, out
         for h in range(2):
             square_and_gain(0, halves[h], ee_early[h][:, :, 0])
             center(1, halves[h], ee_early[h][:, :, 1])
-        rstd_early = deviation(0, lambda d: ee_early[d // 4][:, d % 4].rearrange("p u w -> p (u w)"))
+        rstd_early = deviation(0, lambda d: ee_early[d // 4][:, d % 4].rearrange("p u w -> p (u w)"), "turned0")
         group_sum(2, "total2")
         group_sum(3, "total3")
 
@@ -219,9 +219,9 @@ def tile_picked_ygrp_relu_p_kernel(tc, x_words, x_scales, w1, w2, gam, offs, out
         nc.vector.scalar_tensor_tensor(out=dd2[:], in0=total[2][:].unsqueeze(2).broadcast_to([P, WIDE, D]), scalar=-1.0 / D,
                                        in1=y[2][:].rearrange("p t (v d) -> p (t v) d", d=D), op0=ALU.mult, op1=ALU.add)
         nc.scalar.activation(out=ee2[:], in_=dd2[:], func=ACT.Square)
-        for ds in (slice(0, 2), slice(2, 5), slice(5, D)):
+        for ds in halves:
             center(3, ds, ee3[:, ds.start + 1 : ds.stop + 1])
-        rstd3 = deviation(3, lambda d: ee3[:, d : d + 2].rearrange("p d w -> p (d w)"))[:, WIDE:]
+        rstd3 = deviation(3, lambda d: ee3[:, d : d + 2].rearrange("p d w -> p (d w)"), "bank1_0")[:, WIDE:]
 
         nc.vector.quantize_mx(out=w2_codes[:].bitcast(FP8X4), scales=w2_sc[:], in_=w2_bf[:].rearrange("p c j -> p (c j)"))
         var2 = keep.tile([P, WIDE], F32, name="var2")
@@ -229,19 +229,21 @@ def tile_picked_ygrp_relu_p_kernel(tc, x_words, x_scales, w1, w2, gam, offs, out
         rstd2 = keep.tile([P, WIDE], F32, name="rstd2")
         nc.scalar.activation(out=rstd2[:], in_=var2[:], func=ACT.Abs_reciprocal_sqrt, scale=1.0 / D, bias=EPS)
 
-        z_early = keep.tile([P, HALF, PACK], BF16, name="z_early", align_bytes=64)
-        normalise(gained[0][:], rstd_early[:, :WIDE], z_early[:, :CHUNK, :])
-        normalise(gained[1][:], rstd_early[:, WIDE:], z_early[:, CHUNK:, :])
-        factor2 = keep.tile([P, GROUPS, PACK], F32, name="factor2")
-        nc.vector.tensor_tensor(out=factor2[:], in0=rstd2[:].rearrange("p (t v) -> p v t", t=PACK),
-                                in1=gam_sb[:].unsqueeze(1).broadcast_to([P, GROUPS, PACK]), op=ALU.mult)
-        early_layer(*quantise("z_early", z_early[:]))
+        factor2 = keep.tile([P, PACK, GROUPS], F32, name="factor2")
+        for t in range(PACK):
+            nc.scalar.activation(out=factor2[:, t], in_=rstd2[:, t * GROUPS : (t + 1) * GROUPS], func=ACT.Copy, scale=gam_sb[:, t : t + 1])
+
+        z_early = [keep.tile([P, CHUNK, PACK], BF16, name=f"z{u}", align_bytes=64) for u in range(2)]
+        normalise(gained[0][:], rstd_early[:, :WIDE], z_early[0][:])
+        normalise(gained[1][:], rstd_early[:, WIDE:], z_early[1][:])
+        second_layer(0, "turned3", "(u d v)", *quantise("z0", z_early[0][:]))
         z2 = keep.tile([P, CHUNK, PACK], BF16, name="z2", align_bytes=64)
         nc.vector.tensor_tensor(out=z2[:].rearrange("p (v d) t -> p v d t", d=D), in0=dd2[:].rearrange("p (t v) d -> p v d t", t=PACK),
-                                in1=factor2[:].unsqueeze(2).broadcast_to([P, GROUPS, D, PACK]), op=ALU.mult)
+                                in1=factor2[:].rearrange("p t v -> p v t").unsqueeze(2).broadcast_to([P, GROUPS, D, PACK]), op=ALU.mult)
         z_last = [keep.tile([P, CHUNK // 2, PACK], BF16, name=f"z_last{h}", align_bytes=64) for h in range(2)]
         z_codes = keep.tile([P, CHUNK], U32, name="z_last_codes", align_bytes=64)
         z_sc = keep.tile([P, CHUNK], U8, name="z_last_sc", align_bytes=64)
+        second_layer(CHUNK, "bank0_0", "(u d v)", *quantise("z1", z_early[1][:]))
         second_layer(2 * CHUNK, "bank2_0", "(u v d)", *quantise("z2", z2[:]))
         normalise(gained[3][:, halves[0]], rstd3, z_last[0][:])
         normalise(gained[3][:, halves[1]], rstd3, z_last[1][:])

@@ -108,11 +108,13 @@ def tile_picked_ygrp_relu_p_kernel(tc, x_words, x_scales, w1, w2, gam, offs, out
             count = ds.stop - ds.start
             nc.vector.scalar_tensor_tensor(out=dd[u][:, ds], in0=total[u][:].unsqueeze(1).broadcast_to([P, count, WIDE]), scalar=-1.0 / D,
                                            in1=y[u][:].rearrange("p t (v d) -> p d (t v)", d=D)[:, ds], op0=ALU.mult, op1=ALU.add)
-            square_and_gain(u, ds, squares)
+            square(u, ds, squares)
 
-        def square_and_gain(u, ds, squares):
-            count = ds.stop - ds.start
+        def square(u, ds, squares):
             nc.scalar.activation(out=squares, in_=dd[u][:, ds], func=ACT.Square)
+
+        def take_gain(u, ds):
+            count = ds.stop - ds.start
             nc.gpsimd.tensor_tensor(out=gained[u][:, ds], in0=dd[u][:, ds].rearrange("p d (t v) -> p d v t", t=PACK),
                                     in1=gam_sb[:].unsqueeze(1).unsqueeze(1).broadcast_to([P, count, GROUPS, PACK]), op=ALU.mult)
 
@@ -191,14 +193,14 @@ def tile_picked_ygrp_relu_p_kernel(tc, x_words, x_scales, w1, w2, gam, offs, out
 
         turned_chunks = (0, 1, 3)
         dd = {u: keep.tile([P, D, WIDE], F32, name=f"dd{u}") for u in turned_chunks}
-        for u in turned_chunks:
+        for u in range(2):
             gained[u] = keep.tile([P, D, GROUPS, PACK], F32, name=f"gained{u}")
         halves = [slice(0, D // 2), slice(D // 2, D)]
         ee_early = [keep.tile([P, D // 2, 2, WIDE], F32, name=f"ee_early{h}") for h in range(2)]
         ee3 = keep.tile([P, D + 1, WIDE], F32, name="ee3")
         nc.gpsimd.memset(ee3[:, 0], 0.0)
 
-        w2_bf = keep.tile([P, N, PACK], BF16, name="w2_bf", align_bytes=64)
+        w2_bf = keep.tile([P, N, PACK], BF16, name="w2_bf", tag="w2_bf", align_bytes=64)
         nc.scalar.copy(out=w2_bf[:], in_=w2_raw[:].rearrange("p j c -> p c j"))
 
         total[0] = keep.tile([P, WIDE], F32, name="total0", align_bytes=64)
@@ -208,8 +210,10 @@ def tile_picked_ygrp_relu_p_kernel(tc, x_words, x_scales, w1, w2, gam, offs, out
         group_sum(1, "total1")
         first_center(1)
         for h in range(2):
-            square_and_gain(0, halves[h], ee_early[h][:, :, 0])
+            square(0, halves[h], ee_early[h][:, :, 0])
+            take_gain(0, halves[h])
             center(1, halves[h], ee_early[h][:, :, 1])
+            take_gain(1, halves[h])
         rstd_early = deviation(0, lambda d: ee_early[d // 4][:, d % 4].rearrange("p u w -> p (u w)"), "turned0")
         group_sum(2, "total2")
         group_sum(3, "total3")
@@ -219,19 +223,22 @@ def tile_picked_ygrp_relu_p_kernel(tc, x_words, x_scales, w1, w2, gam, offs, out
         nc.vector.scalar_tensor_tensor(out=dd2[:], in0=total[2][:].unsqueeze(2).broadcast_to([P, WIDE, D]), scalar=-1.0 / D,
                                        in1=y[2][:].rearrange("p t (v d) -> p (t v) d", d=D), op0=ALU.mult, op1=ALU.add)
         nc.scalar.activation(out=ee2[:], in_=dd2[:], func=ACT.Square)
-        for ds in halves:
+        for ds in (slice(0, 2), slice(2, 5), slice(5, D)):
             center(3, ds, ee3[:, ds.start + 1 : ds.stop + 1])
         rstd3 = deviation(3, lambda d: ee3[:, d : d + 2].rearrange("p d w -> p (d w)"), "bank1_0")[:, WIDE:]
 
         nc.vector.quantize_mx(out=w2_codes[:].bitcast(FP8X4), scales=w2_sc[:], in_=w2_bf[:].rearrange("p c j -> p (c j)"))
+        gained[3] = keep.tile([P, D, GROUPS, PACK], F32, name="gained3", tag="w2_bf", align_bytes=64)
+        for ds in halves:
+            take_gain(3, ds)
         var2 = keep.tile([P, WIDE], F32, name="var2")
         nc.vector.tensor_reduce(out=var2[:], in_=ee2[:], axis=AX.X, op=ALU.add)
         rstd2 = keep.tile([P, WIDE], F32, name="rstd2")
         nc.scalar.activation(out=rstd2[:], in_=var2[:], func=ACT.Abs_reciprocal_sqrt, scale=1.0 / D, bias=EPS)
 
-        factor2 = keep.tile([P, PACK, GROUPS], F32, name="factor2")
+        factor2 = keep.tile([P, GROUPS, PACK], F32, name="factor2")
         for t in range(PACK):
-            nc.scalar.activation(out=factor2[:, t], in_=rstd2[:, t * GROUPS : (t + 1) * GROUPS], func=ACT.Copy, scale=gam_sb[:, t : t + 1])
+            nc.scalar.activation(out=factor2[:, :, t], in_=rstd2[:, t * GROUPS : (t + 1) * GROUPS], func=ACT.Copy, scale=gam_sb[:, t : t + 1])
 
         z_early = [keep.tile([P, CHUNK, PACK], BF16, name=f"z{u}", align_bytes=64) for u in range(2)]
         normalise(gained[0][:], rstd_early[:, :WIDE], z_early[0][:])
@@ -239,7 +246,7 @@ def tile_picked_ygrp_relu_p_kernel(tc, x_words, x_scales, w1, w2, gam, offs, out
         second_layer(0, "turned3", "(u d v)", *quantise("z0", z_early[0][:]))
         z2 = keep.tile([P, CHUNK, PACK], BF16, name="z2", align_bytes=64)
         nc.vector.tensor_tensor(out=z2[:].rearrange("p (v d) t -> p v d t", d=D), in0=dd2[:].rearrange("p (t v) d -> p v d t", t=PACK),
-                                in1=factor2[:].rearrange("p t v -> p v t").unsqueeze(2).broadcast_to([P, GROUPS, D, PACK]), op=ALU.mult)
+                                in1=factor2[:].unsqueeze(2).broadcast_to([P, GROUPS, D, PACK]), op=ALU.mult)
         z_last = [keep.tile([P, CHUNK // 2, PACK], BF16, name=f"z_last{h}", align_bytes=64) for h in range(2)]
         z_codes = keep.tile([P, CHUNK], U32, name="z_last_codes", align_bytes=64)
         z_sc = keep.tile([P, CHUNK], U8, name="z_last_sc", align_bytes=64)

@@ -213,7 +213,10 @@ def tile_picked_ygrp_relu_p_kernel(tc, x_words, x_scales, w1, w2, gam, offs, out
             square(0, halves[h], ee_early[h][:, :, 0])
             take_gain(0, halves[h])
             center(1, halves[h], ee_early[h][:, :, 1])
-            take_gain(1, halves[h])
+            if h == 0:
+                take_gain(1, halves[h])
+        take_gain(1, slice(D // 2, 3 * D // 4))
+        take_gain(1, slice(3 * D // 4, D))
         rstd_early = deviation(0, lambda d: ee_early[d // 4][:, d % 4].rearrange("p u w -> p (u w)"), "turned0")
         group_sum(2, "total2")
         group_sum(3, "total3")

@@ -168,15 +168,6 @@ def tile_picked_ygrp_relu_p_kernel(tc, x_words, x_scales, w1, w2, gam, offs, out
                                  in_=acc[:].rearrange(f"p h {order} -> p (h u) v d", v=GROUPS, d=D), func=ACT.Relu)
             nc.sync.dma_start(out=out.rearrange("(h p) j -> p h j", p=P)[:, :, first : first + width], in_=res[:])
 
-        def early_layer(z_codes, z_sc):
-            for h in range(N // P):
-                acc = psum.tile([P, HALF], F32, name=f"acc_early{h}", tag=("turned3", "bank0_1")[h])
-                product(acc[:], h, z_codes, z_sc)
-                res = keep.tile([P, HALF], F32, name=f"res_early{h}")
-                nc.scalar.activation(out=res[:].rearrange("p (u v d) -> p u v d", v=GROUPS, d=D),
-                                     in_=acc[:].rearrange("p (u d v) -> p u v d", v=GROUPS, d=D), func=ACT.Relu)
-                nc.sync.dma_start(out=out[h * P : (h + 1) * P, :HALF], in_=res[:])
-
         def last_layer(first, z_codes, z_sc, tag_low, tag_high):
             last = slice(first, first + CHUNK)
             acc_low = psum.tile([P, CHUNK], F32, name="acc_low", tag=tag_low)
@@ -209,14 +200,12 @@ def tile_picked_ygrp_relu_p_kernel(tc, x_words, x_scales, w1, w2, gam, offs, out
         first_center(0)
         group_sum(1, "total1")
         first_center(1)
+        nc.vector.quantize_mx(out=w2_codes[:].bitcast(FP8X4), scales=w2_sc[:], in_=w2_bf[:].rearrange("p c j -> p (c j)"))
+        take_gain(0, slice(0, D))
         for h in range(2):
             square(0, halves[h], ee_early[h][:, :, 0])
-            take_gain(0, halves[h])
             center(1, halves[h], ee_early[h][:, :, 1])
-            if h == 0:
-                take_gain(1, halves[h])
-        take_gain(1, slice(D // 2, 3 * D // 4))
-        take_gain(1, slice(3 * D // 4, D))
+        take_gain(1, slice(0, D))
         rstd_early = deviation(0, lambda d: ee_early[d // 4][:, d % 4].rearrange("p u w -> p (u w)"), "turned0")
         group_sum(2, "total2")
         group_sum(3, "total3")
@@ -230,10 +219,8 @@ def tile_picked_ygrp_relu_p_kernel(tc, x_words, x_scales, w1, w2, gam, offs, out
             center(3, ds, ee3[:, ds.start + 1 : ds.stop + 1])
         rstd3 = deviation(3, lambda d: ee3[:, d : d + 2].rearrange("p d w -> p (d w)"), "bank1_0")[:, WIDE:]
 
-        nc.vector.quantize_mx(out=w2_codes[:].bitcast(FP8X4), scales=w2_sc[:], in_=w2_bf[:].rearrange("p c j -> p (c j)"))
-        gained[3] = keep.tile([P, D, GROUPS, PACK], F32, name="gained3", tag="w2_bf", align_bytes=64)
-        for ds in halves:
-            take_gain(3, ds)
+        gained[3] = keep.tile([P, D, GROUPS, PACK], F32, name="gained3")
+        take_gain(3, slice(0, D))
         var2 = keep.tile([P, WIDE], F32, name="var2")
         nc.vector.tensor_reduce(out=var2[:], in_=ee2[:], axis=AX.X, op=ALU.add)
         rstd2 = keep.tile([P, WIDE], F32, name="rstd2")

@@ -37,17 +37,14 @@ def tile_picked_ygrp_relu_p_kernel(tc, x_words, x_scales, w1, w2, gam, offs, out
         table_words = keep.tile([P, T], U32, name="table_words", align_bytes=64)
         table_scales = keep.tile([P, T], U8, name="table_scales", tag="scales_then_w2", align_bytes=64)
         w1_raw = keep.tile([P, PACK, H], F32, name="w1_raw", align_bytes=64)
-        gam_sb = keep.tile([P, PACK], F32, name="gam_sb")
 
         nc.gpsimd.memset(table_scales[:].bitcast(I32), 0)
         w1_rows = w1.rearrange("(p j) c -> p j c", j=PACK)
-        nc.sync.dma_start(out=w1_raw[:, :2], in_=w1_rows[:, :2])
+        nc.sync.dma_start(out=w1_raw[:, :1], in_=w1_rows[:, :1])
         nc.sync.dma_start(offsets[:], offs)
-        for q in range(4):
-            nc.sync.dma_start(out=table_scales[32 * q : 32 * q + 4, :].bitcast(I32), in_=x_scales[0, 4 * q : 4 * q + 4].bitcast(I32))
-        nc.sync.dma_start(out=w1_raw[:, 2:], in_=w1_rows[:, 2:])
+        nc.sync.dma_start(out=table_scales[0:P:8, :].bitcast(I32), in_=x_scales[0].bitcast(I32))
+        nc.sync.dma_start(out=w1_raw[:, 1:], in_=w1_rows[:, 1:])
         nc.sync.dma_start(out=table_words[:].bitcast(I32), in_=x_words[0].rearrange("p c r -> p (c r)").bitcast(I32))
-        nc.sync.dma_start(out=gam_sb[:], in_=gam.rearrange("(p t) o -> p (t o)", t=PACK))
 
         identity = keep.tile([P, P], F32, name="identity")
         make_identity(nc, identity[:])
@@ -58,9 +55,15 @@ def tile_picked_ygrp_relu_p_kernel(tc, x_words, x_scales, w1, w2, gam, offs, out
         nc.scalar.activation(out=warm_out[:], in_=warm_in[:], func=ACT.Abs_reciprocal_sqrt)
 
         x_sc = keep.tile([P, S], U8, name="x_sc", align_bytes=64)
-        nc.vector.tensor_copy(x_sc[:], table_scales[:].indirect(offsets[:]))
+        nc.vector.memset(x_sc[:].bitcast(I32), 0)
+        picked_sc = keep.tile([P, S], U8, name="picked_sc", tag="picked_then_gam", align_bytes=64)
+        nc.vector.tensor_copy(picked_sc[:], table_scales[:].indirect(offsets[:]))
+        for q in range(4):
+            nc.sync.dma_start(out=x_sc[32 * q : 32 * q + 4, :].bitcast(I32), in_=picked_sc[32 * q : 32 * q + 32 : 8, :].bitcast(I32))
         w2_raw = keep.tile([P, PACK, N], F32, name="w2_raw", tag="scales_then_w2", align_bytes=64)
         nc.sync.dma_start(out=w2_raw[:], in_=w2.rearrange("(p j) c -> p j c", j=PACK))
+        gam_sb = keep.tile([P, PACK], F32, name="gam_sb", tag="picked_then_gam", align_bytes=64)
+        nc.sync.dma_start(out=gam_sb[:], in_=gam.rearrange("(p t) o -> p (t o)", t=PACK))
 
         w1_bf = keep.tile([P, PACK * P * PACK], BF16, name="w1_bf", align_bytes=64)
         w1_dst = w1_bf[:].rearrange("p (t m j) -> p m t j", t=PACK, j=PACK)
@@ -200,7 +203,6 @@ def tile_picked_ygrp_relu_p_kernel(tc, x_words, x_scales, w1, w2, gam, offs, out
         first_center(0)
         group_sum(1, "total1")
         first_center(1)
-        nc.vector.quantize_mx(out=w2_codes[:].bitcast(FP8X4), scales=w2_sc[:], in_=w2_bf[:].rearrange("p c j -> p (c j)"))
         take_gain(0, slice(0, D))
         for h in range(2):
             square(0, halves[h], ee_early[h][:, :, 0])
@@ -219,7 +221,8 @@ def tile_picked_ygrp_relu_p_kernel(tc, x_words, x_scales, w1, w2, gam, offs, out
             center(3, ds, ee3[:, ds.start + 1 : ds.stop + 1])
         rstd3 = deviation(3, lambda d: ee3[:, d : d + 2].rearrange("p d w -> p (d w)"), "bank1_0")[:, WIDE:]
 
-        gained[3] = keep.tile([P, D, GROUPS, PACK], F32, name="gained3")
+        nc.vector.quantize_mx(out=w2_codes[:].bitcast(FP8X4), scales=w2_sc[:], in_=w2_bf[:].rearrange("p c j -> p (c j)"))
+        gained[3] = keep.tile([P, D, GROUPS, PACK], F32, name="gained3", tag="w2_bf", align_bytes=64)
         take_gain(3, slice(0, D))
         var2 = keep.tile([P, WIDE], F32, name="var2")
         nc.vector.tensor_reduce(out=var2[:], in_=ee2[:], axis=AX.X, op=ALU.add)

@@ -25,6 +25,7 @@ CHUNKS = S // CHUNK
 GROUPS = CHUNK // D
 HALF = S // 2
 W1_VECTOR = 80
+W1_FIRST = 768
 
 
 def tile_picked_ygrp_relu_p_kernel(tc, x_words, x_scales, w1, w2, gam, offs, out):
@@ -38,12 +39,14 @@ def tile_picked_ygrp_relu_p_kernel(tc, x_words, x_scales, w1, w2, gam, offs, out
         table_scales = keep.tile([P, T], U8, name="table_scales", tag="scales_then_w2", align_bytes=64)
         w1_raw = keep.tile([P, PACK, H], F32, name="w1_raw", align_bytes=64)
 
-        nc.gpsimd.memset(table_scales[:].bitcast(I32), 0)
-        w1_rows = w1.rearrange("(p j) c -> p j c", j=PACK)
-        nc.sync.dma_start(out=w1_raw[:, :1], in_=w1_rows[:, :1])
+        nc.gpsimd.memset(table_scales[:, : T // 2].bitcast(I32), 0)
+        nc.vector.memset(table_scales[:, T // 2 :].bitcast(I32), 0)
+        w1_rows = w1.rearrange("(p j) c -> p (j c)", j=PACK)
+        w1_flat = w1_raw[:].rearrange("p j c -> p (j c)")
+        nc.sync.dma_start(out=w1_flat[:, :W1_FIRST], in_=w1_rows[:, :W1_FIRST])
         nc.sync.dma_start(offsets[:], offs)
         nc.sync.dma_start(out=table_scales[0:P:8, :].bitcast(I32), in_=x_scales[0].bitcast(I32))
-        nc.sync.dma_start(out=w1_raw[:, 1:], in_=w1_rows[:, 1:])
+        nc.sync.dma_start(out=w1_flat[:, W1_FIRST:], in_=w1_rows[:, W1_FIRST:])
         nc.sync.dma_start(out=table_words[:].bitcast(I32), in_=x_words[0].rearrange("p c r -> p (c r)").bitcast(I32))
 
         identity = keep.tile([P, P], F32, name="identity")

@@ -39,8 +39,7 @@ def tile_picked_ygrp_relu_p_kernel(tc, x_words, x_scales, w1, w2, gam, offs, out
         table_scales = keep.tile([P, T], U8, name="table_scales", tag="scales_then_w2", align_bytes=64)
         w1_raw = keep.tile([P, PACK, H], F32, name="w1_raw", align_bytes=64)
 
-        nc.gpsimd.memset(table_scales[:, : T // 2].bitcast(I32), 0)
-        nc.vector.memset(table_scales[:, T // 2 :].bitcast(I32), 0)
+        nc.gpsimd.memset(table_scales[:].bitcast(I32), 0)
         w1_rows = w1.rearrange("(p j) c -> p (j c)", j=PACK)
         w1_flat = w1_raw[:].rearrange("p j c -> p (j c)")
         nc.sync.dma_start(out=w1_flat[:, :W1_FIRST], in_=w1_rows[:, :W1_FIRST])

@@ -78,22 +78,21 @@ def tile_picked_ygrp_relu_p_kernel(tc, x_words, x_scales, w1, w2, gam, offs, out
         nc.vector.quantize_mx(out=w1_codes[:].bitcast(FP8X4), scales=w1_sc[:], in_=w1_bf[:])
 
         x_codes = []
-        for h in range(2):
-            g = keep.tile([P, HALF], U32, name=f"x_codes{h}", align_bytes=64)
-            nc.vector.tensor_copy(g[:], table_words[:].indirect(offsets[:, h * HALF // 16 : (h + 1) * HALF // 16]))
-            x_codes.append(g)
+        for first, width in ((0, CHUNK), (CHUNK, CHUNK), (HALF, HALF)):
+            g = keep.tile([P, width], U32, name=f"x_codes{first}", align_bytes=64)
+            nc.vector.tensor_copy(g[:], table_words[:].indirect(offsets[:, first // 16 : (first + width) // 16]))
+            x_codes.extend([g[:, c0 : c0 + CHUNK] for c0 in range(0, width, CHUNK)])
 
         y = []
         for u in range(CHUNKS):
             slots = PACK // 2 if u == 0 else PACK
             banks = [psum.tile([P, slots, CHUNK], F32, name=f"y{u}_{b}", tag=f"bank{u}_{b}") for b in range(PACK // slots)]
-            c0 = u * CHUNK % HALF
             for t in range(PACK):
                 nc.tensor.matmul_mx(
                     out=banks[t // slots][:, t % slots, :],
                     lhsT=w1_codes[:, t * P : (t + 1) * P].bitcast(FP8X4),
                     lhsT_scale=w1_sc[:, t * P : (t + 1) * P],
-                    rhs=x_codes[u * CHUNK // HALF][:, c0 : c0 + CHUNK].bitcast(FP8X4),
+                    rhs=x_codes[u].bitcast(FP8X4),
                     rhs_scale=x_sc[:, u * CHUNK : (u + 1) * CHUNK],
                     start=True, stop=True,
                 )

@@ -83,8 +83,8 @@ def tile_picked_ygrp_relu_p_kernel(tc, x_words, x_scales, w1, w2, gam, offs, out
             nc.vector.tensor_copy(g[:], table_words[:].indirect(offsets[:, first // 16 : (first + width) // 16]))
             x_codes.extend([g[:, c0 : c0 + CHUNK] for c0 in range(0, width, CHUNK)])
 
-        y = []
-        for u in range(CHUNKS):
+        y = {}
+        for u in (0, 1, 3, 2):
             slots = PACK // 2 if u == 0 else PACK
             banks = [psum.tile([P, slots, CHUNK], F32, name=f"y{u}_{b}", tag=f"bank{u}_{b}") for b in range(PACK // slots)]
             for t in range(PACK):
@@ -96,7 +96,7 @@ def tile_picked_ygrp_relu_p_kernel(tc, x_words, x_scales, w1, w2, gam, offs, out
                     rhs_scale=x_sc[:, u * CHUNK : (u + 1) * CHUNK],
                     start=True, stop=True,
                 )
-            y.append(banks if u == 0 else banks[0])
+            y[u] = banks if u == 0 else banks[0]
 
         w2_codes = keep.tile([P, N], U32, name="w2_codes", align_bytes=64)
         w2_sc = keep.tile([P, N], U8, name="w2_sc", align_bytes=64)
@@ -180,9 +180,9 @@ def tile_picked_ygrp_relu_p_kernel(tc, x_words, x_scales, w1, w2, gam, offs, out
             product(acc_high[:], 1, z_codes, z_sc)
             res_low = keep.tile([P, CHUNK], F32, name="res_low")
             res_high = keep.tile([P, CHUNK], F32, name="res_high")
-            nc.scalar.activation(out=res_low[:].rearrange("p (v d) -> p v d", d=D), in_=acc_low[:].rearrange("p (d v) -> p v d", d=D), func=ACT.Relu)
+            nc.scalar.activation(out=res_low[:], in_=acc_low[:], func=ACT.Relu)
             nc.scalar.dma_start(out=out[:P, last], in_=res_low[:])
-            nc.vector.tensor_relu(out=res_high[:].rearrange("p (v d) -> p v d", d=D), in_=acc_high[:].rearrange("p (d v) -> p v d", d=D))
+            nc.vector.tensor_relu(out=res_high[:], in_=acc_high[:])
             nc.sync.dma_start(out=out[P:, last], in_=res_high[:])
 
 
@@ -210,23 +210,26 @@ def tile_picked_ygrp_relu_p_kernel(tc, x_words, x_scales, w1, w2, gam, offs, out
             center(1, halves[h], ee_early[h][:, :, 1])
         take_gain(1, slice(0, D))
         rstd_early = deviation(0, lambda d: ee_early[d // 4][:, d % 4].rearrange("p u w -> p (u w)"), "turned0")
-        group_sum(2, "total2")
         group_sum(3, "total3")
-
-        dd2 = keep.tile([P, WIDE, D], F32, name="dd2")
-        ee2 = keep.tile([P, WIDE, D], F32, name="ee2")
-        nc.vector.scalar_tensor_tensor(out=dd2[:], in0=total[2][:].unsqueeze(2).broadcast_to([P, WIDE, D]), scalar=-1.0 / D,
-                                       in1=y[2][:].rearrange("p t (v d) -> p (t v) d", d=D), op0=ALU.mult, op1=ALU.add)
-        nc.scalar.activation(out=ee2[:], in_=dd2[:], func=ACT.Square)
+        group_sum(2, "total2")
         for ds in (slice(0, 2), slice(2, 5), slice(5, D)):
             center(3, ds, ee3[:, ds.start + 1 : ds.stop + 1])
         rstd3 = deviation(3, lambda d: ee3[:, d : d + 2].rearrange("p d w -> p (d w)"), "bank1_0")[:, WIDE:]
+
+        dd2 = keep.tile([P, WIDE, D], F32, name="dd2")
+        ee2 = keep.tile([P, WIDE, D], F32, name="ee2")
+        pieces = [slice(0, WIDE // 2), slice(WIDE // 2, WIDE)]
+        for ws in pieces:
+            nc.vector.scalar_tensor_tensor(out=dd2[:, ws], in0=total[2][:, ws].unsqueeze(2).broadcast_to([P, WIDE // 2, D]), scalar=-1.0 / D,
+                                           in1=y[2][:].rearrange("p t (v d) -> p (t v) d", d=D)[:, ws], op0=ALU.mult, op1=ALU.add)
+            nc.scalar.activation(out=ee2[:, ws], in_=dd2[:, ws], func=ACT.Square)
 
         nc.vector.quantize_mx(out=w2_codes[:].bitcast(FP8X4), scales=w2_sc[:], in_=w2_bf[:].rearrange("p c j -> p (c j)"))
         gained[3] = keep.tile([P, D, GROUPS, PACK], F32, name="gained3", tag="w2_bf", align_bytes=64)
         take_gain(3, slice(0, D))
         var2 = keep.tile([P, WIDE], F32, name="var2")
-        nc.vector.tensor_reduce(out=var2[:], in_=ee2[:], axis=AX.X, op=ALU.add)
+        for ws in pieces:
+            nc.vector.tensor_reduce(out=var2[:, ws], in_=ee2[:, ws], axis=AX.X, op=ALU.add)
         rstd2 = keep.tile([P, WIDE], F32, name="rstd2")
         nc.scalar.activation(out=rstd2[:], in_=var2[:], func=ACT.Abs_reciprocal_sqrt, scale=1.0 / D, bias=EPS)
 
@@ -238,17 +241,22 @@ def tile_picked_ygrp_relu_p_kernel(tc, x_words, x_scales, w1, w2, gam, offs, out
         normalise(gained[0][:], rstd_early[:, :WIDE], z_early[0][:])
         normalise(gained[1][:], rstd_early[:, WIDE:], z_early[1][:])
         second_layer(0, "turned3", "(u d v)", *quantise("z0", z_early[0][:]))
-        z2 = keep.tile([P, CHUNK, PACK], BF16, name="z2", align_bytes=64)
-        nc.vector.tensor_tensor(out=z2[:].rearrange("p (v d) t -> p v d t", d=D), in0=dd2[:].rearrange("p (t v) d -> p v d t", t=PACK),
-                                in1=factor2[:].unsqueeze(2).broadcast_to([P, GROUPS, D, PACK]), op=ALU.mult)
+        z3 = keep.tile([P, CHUNK, PACK], BF16, name="z3", align_bytes=64)
+        normalise(gained[3][:], rstd3, z3[:])
+        second_layer(CHUNK, "bank0_0", "(u d v)", *quantise("z1", z_early[1][:]))
         z_last = [keep.tile([P, CHUNK // 2, PACK], BF16, name=f"z_last{h}", align_bytes=64) for h in range(2)]
         z_codes = keep.tile([P, CHUNK], U32, name="z_last_codes", align_bytes=64)
         z_sc = keep.tile([P, CHUNK], U8, name="z_last_sc", align_bytes=64)
-        second_layer(CHUNK, "bank0_0", "(u d v)", *quantise("z1", z_early[1][:]))
-        second_layer(2 * CHUNK, "bank2_0", "(u v d)", *quantise("z2", z2[:]))
-        normalise(gained[3][:, halves[0]], rstd3, z_last[0][:])
-        normalise(gained[3][:, halves[1]], rstd3, z_last[1][:])
+
+        def normalise_last(h):
+            vs = slice(h * GROUPS // 2, (h + 1) * GROUPS // 2)
+            nc.vector.tensor_tensor(out=z_last[h][:].rearrange("p (v d) t -> p v d t", d=D), in0=dd2[:].rearrange("p (t v) d -> p v d t", t=PACK)[:, vs],
+                                    in1=factor2[:, vs].unsqueeze(2).broadcast_to([P, GROUPS // 2, D, PACK]), op=ALU.mult)
+
+        second_layer(3 * CHUNK, "bank3_0", "(u d v)", *quantise("z3", z3[:]))
+        normalise_last(0)
+        normalise_last(1)
         for h in range(2):
             cols = slice(h * CHUNK // 2, (h + 1) * CHUNK // 2)
             nc.vector.quantize_mx(out=z_codes[:, cols].bitcast(FP8X4), scales=z_sc[:, cols], in_=z_last[h][:].rearrange("p c t -> p (c t)"))
-        last_layer(3 * CHUNK, z_codes, z_sc, "bank3_0", "bank1_0")
+        last_layer(2 * CHUNK, z_codes, z_sc, "bank2_0", "bank0_1")

@@ -176,8 +176,8 @@ def tile_picked_ygrp_relu_p_kernel(tc, x_words, x_scales, w1, w2, gam, offs, out
             last = slice(first, first + CHUNK)
             acc_low = psum.tile([P, CHUNK], F32, name="acc_low", tag=tag_low)
             acc_high = psum.tile([P, CHUNK], F32, name="acc_high", tag=tag_high)
-            product(acc_low[:], 0, z_codes, z_sc)
             product(acc_high[:], 1, z_codes, z_sc)
+            product(acc_low[:], 0, z_codes, z_sc)
             res_low = keep.tile([P, CHUNK], F32, name="res_low")
             res_high = keep.tile([P, CHUNK], F32, name="res_high")
             nc.scalar.activation(out=res_low[:], in_=acc_low[:], func=ACT.Relu)

@@ -233,9 +233,9 @@ def tile_picked_ygrp_relu_p_kernel(tc, x_words, x_scales, w1, w2, gam, offs, out
         rstd2 = keep.tile([P, WIDE], F32, name="rstd2")
         nc.scalar.activation(out=rstd2[:], in_=var2[:], func=ACT.Abs_reciprocal_sqrt, scale=1.0 / D, bias=EPS)
 
-        factor2 = keep.tile([P, GROUPS, PACK], F32, name="factor2")
+        factor2 = keep.tile([P, PACK, GROUPS, 2], F32, name="factor2")
         for t in range(PACK):
-            nc.scalar.activation(out=factor2[:, :, t], in_=rstd2[:, t * GROUPS : (t + 1) * GROUPS], func=ACT.Copy, scale=gam_sb[:, t : t + 1])
+            nc.scalar.activation(out=factor2[:, t], in_=rstd2[:, t * GROUPS : (t + 1) * GROUPS].unsqueeze(2).broadcast_to([P, GROUPS, 2]), func=ACT.Copy, scale=gam_sb[:, t : t + 1])
 
         z_early = [keep.tile([P, CHUNK, PACK], BF16, name=f"z{u}", align_bytes=64) for u in range(2)]
         normalise(gained[0][:], rstd_early[:, :WIDE], z_early[0][:])
@@ -249,9 +249,9 @@ def tile_picked_ygrp_relu_p_kernel(tc, x_words, x_scales, w1, w2, gam, offs, out
         z_sc = keep.tile([P, CHUNK], U8, name="z_last_sc", align_bytes=64)
 
         def normalise_last(h):
-            vs = slice(h * GROUPS // 2, (h + 1) * GROUPS // 2)
-            nc.vector.tensor_tensor(out=z_last[h][:].rearrange("p (v d) t -> p v d t", d=D), in0=dd2[:].rearrange("p (t v) d -> p v d t", t=PACK)[:, vs],
-                                    in1=factor2[:, vs].unsqueeze(2).broadcast_to([P, GROUPS // 2, D, PACK]), op=ALU.mult)
+            runs = slice(h * GROUPS, (h + 1) * GROUPS)
+            nc.vector.tensor_tensor(out=z_last[h][:].rearrange("p (r i) t -> p r t i", i=4), in0=dd2[:].rearrange("p (t v) (e i) -> p (v e) t i", t=PACK, i=4)[:, runs],
+                                    in1=factor2[:].rearrange("p t v e -> p (v e) t")[:, runs].unsqueeze(3).broadcast_to([P, GROUPS, PACK, 4]), op=ALU.mult)
 
         second_layer(3 * CHUNK, "bank3_0", "(u d v)", *quantise("z3", z3[:]))
         normalise_last(0)

@@ -108,11 +108,10 @@ def tile_picked_ygrp_relu_p_kernel(tc, x_words, x_scales, w1, w2, gam, offs, out
             total[u] = keep.tile([P, WIDE], F32, name=f"total{u}", tag=tag, align_bytes=64)
             nc.vector.tensor_reduce(out=total[u][:], in_=y[u][:].rearrange("p t (v d) -> p (t v) d", d=D), axis=AX.X, op=ALU.add)
 
-        def center(u, ds, squares):
+        def center(u, ds):
             count = ds.stop - ds.start
             nc.vector.scalar_tensor_tensor(out=dd[u][:, ds], in0=total[u][:].unsqueeze(1).broadcast_to([P, count, WIDE]), scalar=-1.0 / D,
                                            in1=y[u][:].rearrange("p t (v d) -> p d (t v)", d=D)[:, ds], op0=ALU.mult, op1=ALU.add)
-            square(u, ds, squares)
 
         def square(u, ds, squares):
             nc.scalar.activation(out=squares, in_=dd[u][:, ds], func=ACT.Square)
@@ -130,11 +129,14 @@ def tile_picked_ygrp_relu_p_kernel(tc, x_words, x_scales, w1, w2, gam, offs, out
             nc.vector.scalar_tensor_tensor(out=dd[0][:, :, cols], in0=total[0][:, cols].unsqueeze(1).broadcast_to([P, D, WIDE // 2]), scalar=-1.0 / D,
                                            in1=y[0][b][:].rearrange("p t (v d) -> p d (t v)", d=D), op0=ALU.mult, op1=ALU.add)
 
-        def deviation(name, columns, back_tag):
+        def add_turned(name, columns):
             turned = psum.tile([P, P], F32, name=f"turned{name}", tag=f"turned{name}")
             for d in range(D):
                 nc.tensor.matmul(out=turned[:], lhsT=columns(d), rhs=identity[:], is_transpose=True, start=(d == 0), stop=(d == D - 1))
-            rstd_turned = keep.tile([P, P], F32, name=f"rstd_turned{name}")
+            return turned
+
+        def deviation(name, turned, root_tag, back_tag):
+            rstd_turned = keep.tile([P, P], F32, name=f"rstd_turned{name}", tag=root_tag, align_bytes=64)
             nc.scalar.activation(out=rstd_turned[:], in_=turned[:], func=ACT.Abs_reciprocal_sqrt, scale=1.0 / D, bias=EPS)
             back = psum.tile([P, P], F32, name=f"back{name}", tag=back_tag)
             nc.tensor.transpose(back[:], rstd_turned[:], identity[:])
@@ -207,14 +209,19 @@ def tile_picked_ygrp_relu_p_kernel(tc, x_words, x_scales, w1, w2, gam, offs, out
         take_gain(0, slice(0, D))
         for h in range(2):
             square(0, halves[h], ee_early[h][:, :, 0])
-            center(1, halves[h], ee_early[h][:, :, 1])
+            center(1, halves[h])
+            square(1, halves[h], ee_early[h][:, :, 1])
         take_gain(1, slice(0, D))
-        rstd_early = deviation(0, lambda d: ee_early[d // 4][:, d % 4].rearrange("p u w -> p (u w)"), "turned0")
+        turned_early = add_turned(0, lambda d: ee_early[d // 4][:, d % 4].rearrange("p u w -> p (u w)"))
         group_sum(3, "total3")
         group_sum(2, "total2")
-        for ds in (slice(0, 2), slice(2, 5), slice(5, D)):
-            center(3, ds, ee3[:, ds.start + 1 : ds.stop + 1])
-        rstd3 = deviation(3, lambda d: ee3[:, d : d + 2].rearrange("p d w -> p (d w)"), "bank1_0")[:, WIDE:]
+        for ds in (slice(0, 2), slice(2, 5)):
+            center(3, ds)
+            square(3, ds, ee3[:, ds.start + 1 : ds.stop + 1])
+        center(3, slice(5, D))
+        rstd_early = deviation(0, turned_early, "total3", "turned0")
+        square(3, slice(5, D), ee3[:, 6:])
+        rstd3 = deviation(3, add_turned(3, lambda d: ee3[:, d : d + 2].rearrange("p d w -> p (d w)")), "root3", "bank1_0")[:, WIDE:]
 
         dd2 = keep.tile([P, WIDE, D], F32, name="dd2")
         ee2 = keep.tile([P, WIDE, D], F32, name="ee2")

@@ -129,6 +129,11 @@ def tile_picked_ygrp_relu_p_kernel(tc, x_words, x_scales, w1, w2, gam, offs, out
             nc.vector.scalar_tensor_tensor(out=dd[0][:, :, cols], in0=total[0][:, cols].unsqueeze(1).broadcast_to([P, D, WIDE // 2]), scalar=-1.0 / D,
                                            in1=y[0][b][:].rearrange("p t (v d) -> p d (t v)", d=D), op0=ALU.mult, op1=ALU.add)
 
+        def first_gain(b):
+            cols = slice(b * WIDE // 2, (b + 1) * WIDE // 2)
+            nc.gpsimd.tensor_tensor(out=gained[0][:, b], in0=dd[0][:, :, cols].rearrange("p d (t v) -> p d v t", t=2),
+                                    in1=gam_sb[:, 2 * b : 2 * b + 2].unsqueeze(1).unsqueeze(1).broadcast_to([P, D, GROUPS, 2]), op=ALU.mult)
+
         def add_turned(name, columns):
             turned = psum.tile([P, P], F32, name=f"turned{name}", tag=f"turned{name}")
             for d in range(D):
@@ -190,8 +195,8 @@ def tile_picked_ygrp_relu_p_kernel(tc, x_words, x_scales, w1, w2, gam, offs, out
 
         turned_chunks = (0, 1, 3)
         dd = {u: keep.tile([P, D, WIDE], F32, name=f"dd{u}") for u in turned_chunks}
-        for u in range(2):
-            gained[u] = keep.tile([P, D, GROUPS, PACK], F32, name=f"gained{u}")
+        gained[0] = keep.tile([P, 2, D, GROUPS, 2], F32, name="gained0")
+        gained[1] = keep.tile([P, D, GROUPS, PACK], F32, name="gained1")
         halves = [slice(0, D // 2), slice(D // 2, D)]
         ee_early = [keep.tile([P, D // 2, 2, WIDE], F32, name=f"ee_early{h}") for h in range(2)]
         ee3 = keep.tile([P, D + 1, WIDE], F32, name="ee3")
@@ -204,9 +209,10 @@ def tile_picked_ygrp_relu_p_kernel(tc, x_words, x_scales, w1, w2, gam, offs, out
         first_sum(0)
         first_sum(1)
         first_center(0)
+        first_gain(0)
         group_sum(1, "total1")
         first_center(1)
-        take_gain(0, slice(0, D))
+        first_gain(1)
         for h in range(2):
             square(0, halves[h], ee_early[h][:, :, 0])
             center(1, halves[h])
@@ -245,7 +251,8 @@ def tile_picked_ygrp_relu_p_kernel(tc, x_words, x_scales, w1, w2, gam, offs, out
             nc.scalar.activation(out=factor2[:, t], in_=rstd2[:, t * GROUPS : (t + 1) * GROUPS].unsqueeze(2).broadcast_to([P, GROUPS, 2]), func=ACT.Copy, scale=gam_sb[:, t : t + 1])
 
         z_early = [keep.tile([P, CHUNK, PACK], BF16, name=f"z{u}", align_bytes=64) for u in range(2)]
-        normalise(gained[0][:], rstd_early[:, :WIDE], z_early[0][:])
+        nc.vector.tensor_tensor(out=z_early[0][:].rearrange("p (d v) (s t) -> p d v s t", v=GROUPS, t=2), in0=gained[0][:].rearrange("p s d v t -> p d v s t"),
+                                in1=rstd_early[:, :WIDE].rearrange("p (s t v) -> p v s t", s=2, t=2).unsqueeze(1).broadcast_to([P, D, GROUPS, 2, 2]), op=ALU.mult)
         normalise(gained[1][:], rstd_early[:, WIDE:], z_early[1][:])
         second_layer(0, "turned3", "(u d v)", *quantise("z0", z_early[0][:]))
         z3 = keep.tile([P, CHUNK, PACK], BF16, name="z3", align_bytes=64)

from contextlib import ExitStack

import concourse.mybir as mybir
from concourse.masks import make_identity

K, T, S, H, N, D = 512, 2048, 512, 512, 256, 8
EPS = 0.1
FLOPS = 2 * K * H * S + 2 * H * N * S

F32 = mybir.dt.float32
BF16 = mybir.dt.bfloat16
I32 = mybir.dt.int32
U32 = mybir.dt.uint32
U16 = mybir.dt.uint16
U8 = mybir.dt.uint8
FP8X4 = mybir.dt.float8_e4m3fn_x4
ALU = mybir.AluOpType
ACT = mybir.ActivationFunctionType
AX = mybir.AxisListType

P = 128
PACK = 4
CHUNK = 128
CHUNKS = S // CHUNK
GROUPS = CHUNK // D
HALF = S // 2
W1_VECTOR = 80
W1_FIRST = 768


def tile_picked_ygrp_relu_p_kernel(tc, x_words, x_scales, w1, w2, gam, offs, out):
    nc = tc.nc
    with ExitStack() as ctx:
        keep = ctx.enter_context(tc.tile_pool(name="keep", bufs=1))
        psum = ctx.enter_context(tc.psum_pool(name="psum", bufs=1))

        offsets = keep.tile([P, S // 16], U16, name="offsets")
        table_words = keep.tile([P, T], U32, name="table_words", align_bytes=64)
        table_scales = keep.tile([P, T], U8, name="table_scales", tag="scales_then_w2", align_bytes=64)
        w1_raw = keep.tile([P, PACK, H], F32, name="w1_raw", align_bytes=64)

        nc.gpsimd.memset(table_scales[:].bitcast(I32), 0)
        w1_rows = w1.rearrange("(p j) c -> p (j c)", j=PACK)
        w1_flat = w1_raw[:].rearrange("p j c -> p (j c)")
        nc.sync.dma_start(out=w1_flat[:, :W1_FIRST], in_=w1_rows[:, :W1_FIRST])
        nc.sync.dma_start(offsets[:], offs)
        nc.sync.dma_start(out=table_scales[0:P:8, :].bitcast(I32), in_=x_scales[0].bitcast(I32))
        nc.sync.dma_start(out=w1_flat[:, W1_FIRST:], in_=w1_rows[:, W1_FIRST:])
        nc.sync.dma_start(out=table_words[:].bitcast(I32), in_=x_words[0].rearrange("p c r -> p (c r)").bitcast(I32))

        identity = keep.tile([P, P], F32, name="identity")
        make_identity(nc, identity[:])

        warm_in = keep.tile([P, 1], F32, name="warm_in")
        warm_out = keep.tile([P, 1], F32, name="warm_out")
        nc.vector.memset(warm_in[:], 1.0)
        nc.scalar.activation(out=warm_out[:], in_=warm_in[:], func=ACT.Abs_reciprocal_sqrt)

        x_sc = keep.tile([P, S], U8, name="x_sc", align_bytes=64)
        nc.vector.memset(x_sc[:].bitcast(I32), 0)
        picked_sc = keep.tile([P, S], U8, name="picked_sc", tag="picked_then_gam", align_bytes=64)
        nc.vector.tensor_copy(picked_sc[:], table_scales[:].indirect(offsets[:]))
        for q in range(4):
            nc.sync.dma_start(out=x_sc[32 * q : 32 * q + 4, :].bitcast(I32), in_=picked_sc[32 * q : 32 * q + 32 : 8, :].bitcast(I32))
        w2_raw = keep.tile([P, PACK, N], F32, name="w2_raw", tag="scales_then_w2", align_bytes=64)
        nc.sync.dma_start(out=w2_raw[:], in_=w2.rearrange("(p j) c -> p j c", j=PACK))
        gam_sb = keep.tile([P, PACK], F32, name="gam_sb", tag="picked_then_gam", align_bytes=64)
        nc.sync.dma_start(out=gam_sb[:], in_=gam.rearrange("(p t) o -> p (t o)", t=PACK))

        w1_bf = keep.tile([P, PACK * P * PACK], BF16, name="w1_bf", align_bytes=64)
        w1_dst = w1_bf[:].rearrange("p (t m j) -> p m t j", t=PACK, j=PACK)
        w1_src = w1_raw[:].rearrange("p j (m t) -> p m t j", t=PACK)
        nc.vector.tensor_copy(out=w1_dst[:, :W1_VECTOR], in_=w1_src[:, :W1_VECTOR])
        nc.scalar.copy(out=w1_dst[:, W1_VECTOR:], in_=w1_src[:, W1_VECTOR:])

        w1_codes = keep.tile([P, H], U32, name="w1_codes", align_bytes=64)
        w1_sc = keep.tile([P, H], U8, name="w1_sc", align_bytes=64)
        nc.vector.quantize_mx(out=w1_codes[:].bitcast(FP8X4), scales=w1_sc[:], in_=w1_bf[:])

        x_codes = []
        for first, width in ((0, CHUNK), (CHUNK, CHUNK), (HALF, HALF)):
            g = keep.tile([P, width], U32, name=f"x_codes{first}", align_bytes=64)
            nc.vector.tensor_copy(g[:], table_words[:].indirect(offsets[:, first // 16 : (first + width) // 16]))
            x_codes.extend([g[:, c0 : c0 + CHUNK] for c0 in range(0, width, CHUNK)])

        y = {}
        for u in (0, 1, 3, 2):
            slots = PACK // 2 if u == 0 else PACK
            banks = [psum.tile([P, slots, CHUNK], F32, name=f"y{u}_{b}", tag=f"bank{u}_{b}") for b in range(PACK // slots)]
            for t in range(PACK):
                nc.tensor.matmul_mx(
                    out=banks[t // slots][:, t % slots, :],
                    lhsT=w1_codes[:, t * P : (t + 1) * P].bitcast(FP8X4),
                    lhsT_scale=w1_sc[:, t * P : (t + 1) * P],
                    rhs=x_codes[u].bitcast(FP8X4),
                    rhs_scale=x_sc[:, u * CHUNK : (u + 1) * CHUNK],
                    start=True, stop=True,
                )
            y[u] = banks if u == 0 else banks[0]

        w2_codes = keep.tile([P, N], U32, name="w2_codes", align_bytes=64)
        w2_sc = keep.tile([P, N], U8, name="w2_sc", align_bytes=64)

        WIDE = GROUPS * PACK
        total, ee, gained = {}, {}, {}

        def group_sum(u, tag):
            total[u] = keep.tile([P, WIDE], F32, name=f"total{u}", tag=tag, align_bytes=64)
            nc.vector.tensor_reduce(out=total[u][:], in_=y[u][:].rearrange("p t (v d) -> p (t v) d", d=D), axis=AX.X, op=ALU.add)

        def center(u, ds):
            count = ds.stop - ds.start
            nc.vector.scalar_tensor_tensor(out=dd[u][:, ds], in0=total[u][:].unsqueeze(1).broadcast_to([P, count, WIDE]), scalar=-1.0 / D,
                                           in1=y[u][:].rearrange("p t (v d) -> p d (t v)", d=D)[:, ds], op0=ALU.mult, op1=ALU.add)

        def square(u, ds, squares):
            nc.scalar.activation(out=squares, in_=dd[u][:, ds], func=ACT.Square)

        def take_gain(u, ds):
            count = ds.stop - ds.start
            nc.gpsimd.tensor_tensor(out=gained[u][:, ds], in0=dd[u][:, ds].rearrange("p d (t v) -> p d v t", t=PACK),
                                    in1=gam_sb[:].unsqueeze(1).unsqueeze(1).broadcast_to([P, count, GROUPS, PACK]), op=ALU.mult)

        def first_sum(b):
            nc.vector.tensor_reduce(out=total[0][:, b * WIDE // 2 : (b + 1) * WIDE // 2], in_=y[0][b][:].rearrange("p t (v d) -> p (t v) d", d=D), axis=AX.X, op=ALU.add)

        def first_center(b):
            cols = slice(b * WIDE // 2, (b + 1) * WIDE // 2)
            nc.vector.scalar_tensor_tensor(out=dd[0][:, :, cols], in0=total[0][:, cols].unsqueeze(1).broadcast_to([P, D, WIDE // 2]), scalar=-1.0 / D,
                                           in1=y[0][b][:].rearrange("p t (v d) -> p d (t v)", d=D), op0=ALU.mult, op1=ALU.add)

        def first_gain(b):
            cols = slice(b * WIDE // 2, (b + 1) * WIDE // 2)
            nc.gpsimd.tensor_tensor(out=gained[0][:, b], in0=dd[0][:, :, cols].rearrange("p d (t v) -> p d v t", t=2),
                                    in1=gam_sb[:, 2 * b : 2 * b + 2].unsqueeze(1).unsqueeze(1).broadcast_to([P, D, GROUPS, 2]), op=ALU.mult)

        def add_turned(name, columns):
            turned = psum.tile([P, P], F32, name=f"turned{name}", tag=f"turned{name}")
            for d in range(D):
                nc.tensor.matmul(out=turned[:], lhsT=columns(d), rhs=identity[:], is_transpose=True, start=(d == 0), stop=(d == D - 1))
            return turned

        def deviation(name, turned, root_tag, back_tag):
            rstd_turned = keep.tile([P, P], F32, name=f"rstd_turned{name}", tag=root_tag, align_bytes=64)
            nc.scalar.activation(out=rstd_turned[:], in_=turned[:], func=ACT.Abs_reciprocal_sqrt, scale=1.0 / D, bias=EPS)
            back = psum.tile([P, P], F32, name=f"back{name}", tag=back_tag)
            nc.tensor.transpose(back[:], rstd_turned[:], identity[:])
            return back[:]

        def normalise(values, rstd, z):
            count = values.shape[1]
            nc.vector.tensor_tensor(out=z.rearrange("p (d v) t -> p d v t", v=GROUPS), in0=values,
                                    in1=rstd.rearrange("p (t v) -> p v t", t=PACK).unsqueeze(1).broadcast_to([P, count, GROUPS, PACK]), op=ALU.mult)

        def quantise(name, z):
            width = z.shape[1]
            z_codes = keep.tile([P, width], U32, name=f"{name}_codes", align_bytes=64)
            z_sc = keep.tile([P, width], U8, name=f"{name}_sc", align_bytes=64)
            nc.vector.quantize_mx(out=z_codes[:].bitcast(FP8X4), scales=z_sc[:], in_=z.rearrange("p c t -> p (c t)"))
            return z_codes, z_sc

        def product(acc, h, z_codes, z_sc):
            nc.tensor.matmul_mx(
                out=acc,
                lhsT=w2_codes[:, h * P : (h + 1) * P].bitcast(FP8X4),
                lhsT_scale=w2_sc[:, h * P : (h + 1) * P],
                rhs=z_codes[:].bitcast(FP8X4),
                rhs_scale=z_sc[:],
                start=True, stop=True,
            )

        def second_layer(first, tag, order, z_codes, z_sc):
            width = z_codes.shape[1]
            acc = psum.tile([P, N // P, width], F32, name=f"acc{first}", tag=tag)
            for h in range(N // P):
                product(acc[:, h, :], h, z_codes, z_sc)
            res = keep.tile([P, N // P, width], F32, name=f"res{first}")
            nc.scalar.activation(out=res[:].rearrange("p h (u v d) -> p (h u) v d", v=GROUPS, d=D),
                                 in_=acc[:].rearrange(f"p h {order} -> p (h u) v d", v=GROUPS, d=D), func=ACT.Relu)
            nc.sync.dma_start(out=out.rearrange("(h p) j -> p h j", p=P)[:, :, first : first + width], in_=res[:])

        def last_layer(first, z_codes, z_sc, tag_low, tag_high):
            last = slice(first, first + CHUNK)
            acc_low = psum.tile([P, CHUNK], F32, name="acc_low", tag=tag_low)
            acc_high = psum.tile([P, CHUNK], F32, name="acc_high", tag=tag_high)
            product(acc_high[:], 1, z_codes, z_sc)
            product(acc_low[:], 0, z_codes, z_sc)
            res_low = keep.tile([P, CHUNK], F32, name="res_low")
            res_high = keep.tile([P, CHUNK], F32, name="res_high")
            nc.scalar.activation(out=res_low[:], in_=acc_low[:], func=ACT.Relu)
            nc.scalar.dma_start(out=out[:P, last], in_=res_low[:])
            nc.vector.tensor_relu(out=res_high[:], in_=acc_high[:])
            nc.sync.dma_start(out=out[P:, last], in_=res_high[:])


        turned_chunks = (0, 1, 3)
        dd = {u: keep.tile([P, D, WIDE], F32, name=f"dd{u}") for u in turned_chunks}
        gained[0] = keep.tile([P, 2, D, GROUPS, 2], F32, name="gained0")
        gained[1] = keep.tile([P, D, GROUPS, PACK], F32, name="gained1")
        halves = [slice(0, D // 2), slice(D // 2, D)]
        ee_early = [keep.tile([P, D // 2, 2, WIDE], F32, name=f"ee_early{h}") for h in range(2)]
        ee3 = keep.tile([P, D + 1, WIDE], F32, name="ee3")
        nc.gpsimd.memset(ee3[:, 0], 0.0)

        w2_bf = keep.tile([P, N, PACK], BF16, name="w2_bf", tag="w2_bf", align_bytes=64)
        nc.scalar.copy(out=w2_bf[:], in_=w2_raw[:].rearrange("p j c -> p c j"))

        total[0] = keep.tile([P, WIDE], F32, name="total0", align_bytes=64)
        first_sum(0)
        first_sum(1)
        first_center(0)
        first_gain(0)
        group_sum(1, "total1")
        first_center(1)
        first_gain(1)
        for h in range(2):
            square(0, halves[h], ee_early[h][:, :, 0])
            center(1, halves[h])
            square(1, halves[h], ee_early[h][:, :, 1])
        take_gain(1, slice(0, D))
        turned_early = add_turned(0, lambda d: ee_early[d // 4][:, d % 4].rearrange("p u w -> p (u w)"))
        group_sum(3, "total3")
        group_sum(2, "total2")
        for ds in (slice(0, 2), slice(2, 5)):
            center(3, ds)
            square(3, ds, ee3[:, ds.start + 1 : ds.stop + 1])
        center(3, slice(5, D))
        rstd_early = deviation(0, turned_early, "total3", "turned0")
        square(3, slice(5, D), ee3[:, 6:])
        rstd3 = deviation(3, add_turned(3, lambda d: ee3[:, d : d + 2].rearrange("p d w -> p (d w)")), "root3", "bank1_0")[:, WIDE:]

        dd2 = keep.tile([P, WIDE, D], F32, name="dd2")
        ee2 = keep.tile([P, WIDE, D], F32, name="ee2")
        pieces = [slice(0, WIDE // 2), slice(WIDE // 2, WIDE)]
        for ws in pieces:
            nc.vector.scalar_tensor_tensor(out=dd2[:, ws], in0=total[2][:, ws].unsqueeze(2).broadcast_to([P, WIDE // 2, D]), scalar=-1.0 / D,
                                           in1=y[2][:].rearrange("p t (v d) -> p (t v) d", d=D)[:, ws], op0=ALU.mult, op1=ALU.add)
            nc.scalar.activation(out=ee2[:, ws], in_=dd2[:, ws], func=ACT.Square)

        nc.vector.quantize_mx(out=w2_codes[:].bitcast(FP8X4), scales=w2_sc[:], in_=w2_bf[:].rearrange("p c j -> p (c j)"))
        gained[3] = keep.tile([P, D, GROUPS, PACK], F32, name="gained3", tag="w2_bf", align_bytes=64)
        take_gain(3, slice(0, D))
        var2 = keep.tile([P, WIDE], F32, name="var2")
        for ws in pieces:
            nc.vector.tensor_reduce(out=var2[:, ws], in_=ee2[:, ws], axis=AX.X, op=ALU.add)
        rstd2 = keep.tile([P, WIDE], F32, name="rstd2")
        nc.scalar.activation(out=rstd2[:], in_=var2[:], func=ACT.Abs_reciprocal_sqrt, scale=1.0 / D, bias=EPS)

        factor2 = keep.tile([P, PACK, GROUPS, 2], F32, name="factor2")
        for t in range(PACK):
            nc.scalar.activation(out=factor2[:, t], in_=rstd2[:, t * GROUPS : (t + 1) * GROUPS].unsqueeze(2).broadcast_to([P, GROUPS, 2]), func=ACT.Copy, scale=gam_sb[:, t : t + 1])

        z_early = [keep.tile([P, CHUNK, PACK], BF16, name=f"z{u}", align_bytes=64) for u in range(2)]
        nc.vector.tensor_tensor(out=z_early[0][:].rearrange("p (d v) (s t) -> p d v s t", v=GROUPS, t=2), in0=gained[0][:].rearrange("p s d v t -> p d v s t"),
                                in1=rstd_early[:, :WIDE].rearrange("p (s t v) -> p v s t", s=2, t=2).unsqueeze(1).broadcast_to([P, D, GROUPS, 2, 2]), op=ALU.mult)
        normalise(gained[1][:], rstd_early[:, WIDE:], z_early[1][:])
        second_layer(0, "turned3", "(u d v)", *quantise("z0", z_early[0][:]))
        z3 = keep.tile([P, CHUNK, PACK], BF16, name="z3", align_bytes=64)
        normalise(gained[3][:], rstd3, z3[:])
        second_layer(CHUNK, "bank0_0", "(u d v)", *quantise("z1", z_early[1][:]))
        z_last = [keep.tile([P, CHUNK // 2, PACK], BF16, name=f"z_last{h}", align_bytes=64) for h in range(2)]
        z_codes = keep.tile([P, CHUNK], U32, name="z_last_codes", align_bytes=64)
        z_sc = keep.tile([P, CHUNK], U8, name="z_last_sc", align_bytes=64)

        def normalise_last(h):
            runs = slice(h * GROUPS, (h + 1) * GROUPS)
            nc.vector.tensor_tensor(out=z_last[h][:].rearrange("p (r i) t -> p r t i", i=4), in0=dd2[:].rearrange("p (t v) (e i) -> p (v e) t i", t=PACK, i=4)[:, runs],
                                    in1=factor2[:].rearrange("p t v e -> p (v e) t")[:, runs].unsqueeze(3).broadcast_to([P, GROUPS, PACK, 4]), op=ALU.mult)

        second_layer(3 * CHUNK, "bank3_0", "(u d v)", *quantise("z3", z3[:]))
        normalise_last(0)
        normalise_last(1)
        for h in range(2):
            cols = slice(h * CHUNK // 2, (h + 1) * CHUNK // 2)
            nc.vector.quantize_mx(out=z_codes[:, cols].bitcast(FP8X4), scales=z_sc[:, cols], in_=z_last[h][:].rearrange("p c t -> p (c t)"))
        last_layer(2 * CHUNK, z_codes, z_sc, "bank2_0", "bank0_1")
